import numpy as np
import ml_dtypes


def mxq(x, axis, fmt="e4m3"):
    dtype, down = {"e4m3": (ml_dtypes.float8_e4m3fn, 7), "e5m2": (ml_dtypes.float8_e5m2, 14)}[fmt]
    v = np.moveaxis(np.asarray(x, np.float32).astype(ml_dtypes.bfloat16).astype(np.float64), axis, -1)
    blocks = v.reshape(v.shape[:-1] + (-1, 32))
    amax = np.abs(blocks).max(-1, keepdims=True)
    byte = np.maximum(np.where(amax > 0, np.frexp(amax)[1] - 1 + 127, 0) - down, 1)
    scale = np.exp2(byte - 127.0)
    codes = (blocks / scale).astype(np.float32).astype(dtype).astype(np.float64)
    return np.moveaxis((codes * scale).reshape(v.shape), -1, axis)


WIDE = False


def mx_kscale(k):
    if not WIDE:
        return np.ones(k)
    levels = np.array([10, -10, 5, -5, 0])
    if k % 512:
        return np.exp2(np.random.permutation(np.resize(levels, k // 32))).repeat(32)
    a = np.empty((k // 512, 16))
    for p in range(k // 512):
        a[p, :8] = np.random.permutation(np.resize(levels, 8))
        for g in range(8):
            far = levels[np.abs(levels - a[p, g]) >= 10]
            a[p, g + 8] = far[np.random.randint(len(far))]
    return np.exp2(a.ravel()).repeat(32)


BF16 = ml_dtypes.bfloat16


def bf(x):
    return np.asarray(x, np.float32).astype(BF16)


def f64(x):
    return np.asarray(x).astype(np.float64)


E2M1 = np.array([0.0, 0.5, 1.0, 1.5, 2.0, 3.0, 4.0, 6.0, -0.0, -0.5, -1.0, -1.5, -2.0, -3.0, -4.0, -6.0])


def pack_weight(w, fmt):
    k, n = w.shape
    w = f64(bf(w)).reshape(k // 32, 32, n)
    amax = np.abs(w).max(1)
    if fmt == "e4m3":
        byte = np.frexp(amax)[1] - 1 + 127 - 7
    else:
        mant, ex = np.frexp(amax / 6.0)
        byte = np.where(mant > 0.5, ex, ex - 1) + 127
    byte = np.clip(np.where(amax > 0, byte, 1), 1, 254)
    scaled = (w * np.exp2(127.0 - byte)[:, None, :]).reshape(k, n).astype(np.float32)
    by_word = np.ascontiguousarray(scaled.reshape(k // 512, 128, 4, n).transpose(0, 1, 3, 2))
    if fmt == "e4m3":
        words = by_word.astype(ml_dtypes.float8_e4m3fn).view(np.uint8)
    else:
        c = by_word.astype(ml_dtypes.float4_e2m1fn).view(np.uint8) & 0xF
        words = c[..., 0::2] | (c[..., 1::2] << 4)
    return np.ascontiguousarray(words), np.ascontiguousarray(byte.astype(np.uint8).reshape(k // 512, 16, n))


def unpack_weight(words, scales, fmt):
    g, p, n, _ = words.shape
    if fmt == "e4m3":
        vals = np.ascontiguousarray(words).view(ml_dtypes.float8_e4m3fn).astype(np.float64)
    else:
        nib = np.empty((g, p, n, 4), np.uint8)
        nib[..., 0::2] = words & 0xF
        nib[..., 1::2] = words >> 4
        vals = E2M1[nib]
    vals = vals * np.repeat(np.exp2(scales.astype(np.float64) - 127.0), 8, axis=1)[..., None]
    return vals.transpose(0, 1, 3, 2).reshape(g * 512, n)
def pack4(w):
    words, scales = pack_weight(w, "e2m1")
    return words.reshape(words.shape[0], 128, -1), scales


def unpack4(words, scales):
    return unpack_weight(words.reshape(words.shape[0], 128, -1, 2), scales, "e2m1")


E4M3FN = np.array([(-1.0 if i & 128 else 1.0) * ((1.0 + (i & 7) / 8.0) * 2.0 ** (((i >> 3) & 15) - 7) if i & 120 else (i & 7) * 2.0 ** -9) for i in range(256)])


def e4m3fn_bytes(y):
    return np.clip(np.asarray(y, np.float64), -448.0, 448.0).astype(np.float32).astype(ml_dtypes.float8_e4m3fn).view(np.uint8)


def e4m3fn_values(b):
    return E4M3FN[b]


T, C, D, R, B = 2048, 1024, 512, 512, 128


def blocks(scale):
    return np.repeat(np.repeat(f64(scale), B, axis=0), B, axis=1)


def setup_inputs():
    s, u = mx_kscale(C), mx_kscale(T)
    spread = blocks(np.exp(0.5 * np.random.standard_normal((3 * D // B, C // B))))
    w = np.random.standard_normal((3 * D, C)) / np.sqrt(C) * spread / s
    w_scale = (np.abs(w).reshape(3 * D // B, B, C // B, B).max(axis=(1, 3)) / 448).astype(np.float32)
    w_bytes = e4m3fn_bytes(w / blocks(w_scale))
    e_words, e_scales = pack4(np.random.standard_normal((T, R)) / np.sqrt(T) / u[:, None])
    return {"x": bf(np.random.standard_normal((T, C)) * s),
            "w_bytes": w_bytes, "w_scale": w_scale,
            "bias": bf(0.4 * np.random.standard_normal(3 * D)),
            "gain": bf((1 + 0.1 * np.random.standard_normal(T)) * u),
            "e_words": e_words, "e_scales": e_scales}


def reference(x, w_bytes, w_scale, bias, gain, e_words, e_scales):
    w = e4m3fn_values(w_bytes) * np.repeat(np.repeat(f64(w_scale), B, axis=0), B, axis=1)
    h = (mxq(f64(x), 1, "e4m3") @ mxq(w, 1, "e4m3").T) + f64(bias)
    kv = h[:, D:] * f64(gain)[:, None]
    e = unpack4(e_words, e_scales)
    z = e.T @ mxq(kv, 0, "e4m3")
    return h[:, :D], z[:, :D], z[:, D:]

@@ -1,0 +1,580 @@
+from contextlib import ExitStack
+
+import concourse.mybir as mybir
+from concourse.masks import make_identity
+
+T, C, D, R = 2048, 1024, 512, 512
+FLOPS = 2 * T * C * 3 * D + 2 * R * T * 2 * D
+
+F32 = mybir.dt.float32
+BF16 = mybir.dt.bfloat16
+I32 = mybir.dt.int32
+U32 = mybir.dt.uint32
+U8 = mybir.dt.uint8
+FP8 = mybir.dt.float8_e4m3fn
+FP8X4 = mybir.dt.float8_e4m3fn_x4
+FP4X4 = mybir.dt.float4_e2m1fn_x4
+ADD = mybir.AluOpType.add
+MULT = mybir.AluOpType.mult
+COPY = mybir.ActivationFunctionType.Copy
+
+P = 128
+KP = 512
+GROUPS = T // KP
+PASSES = C // KP
+W_TILES = 3 * D // P
+BLOCKS = C // P
+
+
+def tile_qkv_token_compression_d4_kernel(
+    tc, x, w_bytes, w_scale, bias, gain, e_words, e_scales, out_q, out_k, out_v
+):
+    nc = tc.nc
+    with ExitStack() as ctx:
+        keep = ctx.enter_context(tc.tile_pool(name="keep", bufs=1))
+        stage = ctx.enter_context(tc.tile_pool(name="stage", bufs=3))
+        psum = ctx.enter_context(tc.psum_pool(name="psum", bufs=8))
+        ctx.enter_context(tc.manual_schedule())
+
+        ident = keep.tile([P, P], F32, name="ident")
+        pick = keep.tile([P, 8], BF16, name="pick")
+        ones = keep.tile([P, KP], BF16, name="ones")
+        rows = keep.tile([P, T + D + P], BF16, name="rows")
+        gain_all = keep.tile([P, T], BF16, name="gain_all")
+        bias_q = keep.tile([P, D], BF16, name="bias_q")
+        bias_kv = keep.tile([P, 8], F32, name="bias_kv")
+        scale_all = keep.tile([P, W_TILES * BLOCKS], F32, name="scale_all")
+        e_codes = keep.tile([P, GROUPS, 2 * R], U8, name="e_codes", align_bytes=64)
+        e_plane = keep.tile([P, GROUPS, R], U8, name="e_plane", align_bytes=64)
+        x_codes = keep.tile([P, GROUPS, PASSES, KP], U32, name="x_codes", align_bytes=64)
+        x_plane = keep.tile([P, GROUPS, PASSES, KP], U8, name="x_plane", align_bytes=64)
+        wkv_codes = keep.tile([P, 8, PASSES, P], U32, name="wkv_codes", align_bytes=64)
+        wkv_plane = keep.tile([P, 8, PASSES, P], U8, name="wkv_plane", align_bytes=64)
+        wq_grouped = keep.tile([P, PASSES, D, 2], F32, name="wq_grouped", align_bytes=64)
+        wq_codes = keep.tile([P, PASSES, D], U32, name="wq_codes", align_bytes=64)
+        wq_plane = keep.tile([P, PASSES, D], U8, name="wq_plane", align_bytes=64)
+        kv_codes = keep.tile([P, GROUPS, 2, D], U32, name="kv_codes", align_bytes=64)
+        kv_plane = keep.tile([P, GROUPS, 2, D], U8, name="kv_plane", align_bytes=64)
+
+        x_raw, w_raw, x_sorted, w_wide, banks, grouped, kv_rows, q_out = {}, {}, {}, {}, {}, {}, {}, {}
+
+        def load_x(g, k, first, count):
+            if (g, k) not in x_raw:
+                x_raw[g, k] = keep.tile([P, 4, KP], BF16, name="x_raw_%d_%d" % (g, k))
+            src = x[g * KP : (g + 1) * KP, k * KP : (k + 1) * KP].rearrange("(p t) c -> p t c", t=4)
+            nc.sync.dma_start(out=x_raw[g, k][:, first : first + count], in_=src[:, first : first + count])
+
+        def load_w(first, count):
+            tile = keep.tile([P, count, C], U8, name="w_raw_%d" % first)
+            src = w_bytes[first * P : (first + count) * P, :].rearrange("(i p) c -> p i c", p=P)
+            nc.sync.dma_start(out=tile[:], in_=src)
+            for i in range(count):
+                w_raw[first + i] = tile[:, i, :]
+
+        def empty(step, out, in_):
+            if step in EMPTY_ON_VECTOR:
+                nc.vector.tensor_copy(out=out, in_=in_)
+            else:
+                nc.scalar.copy(out=out, in_=in_)
+
+        def widen(i):
+            on_vector = WIDEN_ON_VECTOR[i]
+            wide = stage.tile([P, C], BF16, name="w_wide", bufs=6)
+            w_wide[i] = wide
+            for j in range(BLOCKS):
+                cols = slice(j * P, (j + 1) * P)
+                scale = scale_all[:, i * BLOCKS + j : i * BLOCKS + j + 1]
+                if j < on_vector:
+                    k, b = divmod(j, 4)
+                    dst = wide[:, k * KP : (k + 1) * KP].rearrange("p (u q e) -> p q u e", u=2, e=2)
+                    nc.vector.tensor_scalar(
+                        out=dst[:, 32 * b : 32 * (b + 1)],
+                        in0=w_raw[i][:, cols].bitcast(FP8).rearrange("p (q u e) -> p q u e", u=2, e=2),
+                        scalar1=scale,
+                        scalar2=None,
+                        op0=MULT,
+                    )
+                else:
+                    nc.scalar.activation(out=wide[:, cols], in_=w_raw[i][:, cols].bitcast(FP8), func=COPY, scale=scale)
+
+        def turn_w(i):
+            bank = psum.tile([P, PASSES, 2, P], F32, name="bank")
+            banks["w", i] = bank
+            words = w_wide[i][:].bitcast(F32)
+            for k in range(PASSES):
+                for u in range(2):
+                    if 4 * k < WIDEN_ON_VECTOR[i]:
+                        src = words[:, 256 * k + P * u : 256 * k + P * (u + 1)]
+                    else:
+                        src = words[:, 256 * k + u : 256 * (k + 1) : 2]
+                    nc.tensor.transpose(bank[:, k, u, :], src, ident[:])
+
+        def empty_w(i):
+            src = banks["w", i][:].rearrange("p k u n -> p k n u")
+            if i < 4:
+                empty(("ew", i), wq_grouped[:, :, i * P : (i + 1) * P, :], src)
+            else:
+                tile = stage.tile([P, PASSES, P, 2], F32, name="w_grouped", align_bytes=64)
+                grouped["w", i] = tile
+                empty(("ew", i), tile[:], src)
+
+        def quant_w(i):
+            nc.vector.quantize_mx(
+                out=wkv_codes[:, i - 4].rearrange("p k n -> p (k n)").bitcast(FP8X4),
+                scales=wkv_plane[:, i - 4].rearrange("p k n -> p (k n)"),
+                in_=grouped["w", i][:].rearrange("p k n u -> p (k n u)").bitcast(BF16),
+            )
+
+        def quant_wq(k):
+            nc.vector.quantize_mx(
+                out=wq_codes[:, k, :].bitcast(FP8X4),
+                scales=wq_plane[:, k, :],
+                in_=wq_grouped[:, k].rearrange("p n u -> p (n u)").bitcast(BF16),
+            )
+
+        def sort_x(g, k):
+            tile = stage.tile([P, 4, 2, P], F32, name="x_sorted")
+            x_sorted[g, k] = tile
+            words = x_raw[g, k][:].rearrange("p t c -> p (t c)").bitcast(F32)
+            nc.scalar.copy(out=tile[:], in_=words.rearrange("p (t q u) -> p t u q", t=4, u=2))
+
+        def turn_x(g, k, h):
+            bank = psum.tile([P, 2, 2, P], F32, name="bank")
+            banks["x", g, k, h] = bank
+            for e in range(2):
+                for u in range(2):
+                    if (g, k) in x_sorted:
+                        src = x_sorted[g, k][:, 2 * h + e, u, :]
+                    else:
+                        src = x_raw[g, k][:, 2 * h + e, :].bitcast(F32)[:, u:256:2]
+                    nc.tensor.transpose(bank[:, e, u, :], src, ident[:])
+
+        def empty_x(g, k, h):
+            if ("x", g, k) not in grouped:
+                grouped["x", g, k] = stage.tile([P, 2, P, 4], F32, name="grouped", bufs=4, align_bytes=64)
+            empty(("ex", g, k, h), grouped["x", g, k][:, h], banks["x", g, k, h][:].rearrange("q e u p -> q p (e u)"))
+
+        def quant_x(g, k):
+            nc.vector.quantize_mx(
+                out=x_codes[:, g, k, :].bitcast(FP8X4),
+                scales=x_plane[:, g, k, :],
+                in_=grouped["x", g, k][:].rearrange("q h p w -> q (h p w)").bitcast(BF16),
+            )
+
+        def mul_kv(g, c):
+            bank = psum.tile([P, KP], F32, name="bank")
+            banks["kv", g, c] = bank
+            for k in range(PASSES):
+                nc.tensor.matmul_mx(
+                    out=bank[:],
+                    lhsT=wkv_codes[:, c, k, :].bitcast(FP8X4),
+                    lhsT_scale=wkv_plane[:, c, k, :],
+                    rhs=x_codes[:, g, k, :].bitcast(FP8X4),
+                    rhs_scale=x_plane[:, g, k, :],
+                    start=(k == 0),
+                    stop=(k == PASSES - 1),
+                )
+
+        def empty_kv(g, c):
+            tile = stage.tile([P, KP], BF16, name="kv_rows", bufs=KV_BUFS)
+            kv_rows[g, c] = tile
+            nc.vector.scalar_tensor_tensor(
+                out=tile[:],
+                in0=banks["kv", g, c][:],
+                scalar=bias_kv[:, c : c + 1],
+                in1=gain_all[:, g * KP : (g + 1) * KP],
+                op0=ADD,
+                op1=MULT,
+            )
+
+        def turn_kv(g, pair):
+            bank = psum.tile([P, 2, 2, P], F32, name="bank")
+            banks["t", g, pair] = bank
+            for i in range(2):
+                words = kv_rows[g, 2 * pair + i][:].bitcast(F32)
+                for h in range(2):
+                    nc.tensor.transpose(bank[:, i, h, :], words[:, h * P : (h + 1) * P], ident[:])
+
+        def empty_turned_kv(g, pair):
+            if ("kv", g, pair // 2) not in grouped:
+                grouped["kv", g, pair // 2] = stage.tile([P, 4, P, 2], F32, name="grouped", bufs=4, align_bytes=64)
+            lo = 2 * (pair % 2)
+            empty(("et", g, pair), grouped["kv", g, pair // 2][:, lo : lo + 2], banks["t", g, pair][:].rearrange("p i h n -> p i n h"))
+
+        def quant_kv(g, half):
+            nc.vector.quantize_mx(
+                out=kv_codes[:, g, half, :].bitcast(FP8X4),
+                scales=kv_plane[:, g, half, :],
+                in_=grouped["kv", g, half][:].rearrange("p i n h -> p (i n h)").bitcast(BF16),
+            )
+
+        def mul_q(g, j):
+            bank = psum.tile([P, D], F32, name="bank")
+            banks["q", g, j] = bank
+            for k in range(PASSES):
+                nc.tensor.matmul_mx(
+                    out=bank[:],
+                    lhsT=x_codes[:, g, k, j * P : (j + 1) * P].bitcast(FP8X4),
+                    lhsT_scale=x_plane[:, g, k, j * P : (j + 1) * P],
+                    rhs=wq_codes[:, k, :].bitcast(FP8X4),
+                    rhs_scale=wq_plane[:, k, :],
+                    start=(k == 0),
+                    stop=(k == PASSES - 1),
+                )
+
+        def empty_q(g, j):
+            h, half = divmod(j, 2)
+            first = (g, h) not in q_out
+            if first:
+                q_out[g, h] = stage.tile([P, 2, D], F32, name="q_out", bufs=3)
+            nc.vector.tensor_tensor(out=q_out[g, h][:, half, :], in0=banks["q", g, j][:], in1=bias_q[:], op=ADD)
+            if not first:
+                dst = out_q[g * KP : (g + 1) * KP, :].rearrange("(a p h e) n -> h e p a n", a=2, h=2, e=2)
+                for e in range(2):
+                    nc.sync.dma_start(out=dst[h, e], in_=q_out[g, h][e:P:2])
+
+        def mul_z(half, r):
+            bank = psum.tile([P, D], F32, name="bank")
+            banks["z", half, r] = bank
+            for g in range(GROUPS):
+                nc.tensor.matmul_mx(
+                    out=bank[:],
+                    lhsT=e_codes[:, g, 2 * r * P : 2 * (r + 1) * P].bitcast(FP4X4),
+                    lhsT_scale=e_plane[:, g, r * P : (r + 1) * P],
+                    rhs=kv_codes[:, g, half, :].bitcast(FP8X4),
+                    rhs_scale=kv_plane[:, g, half, :],
+                    start=(g == 0),
+                    stop=(g == GROUPS - 1),
+                )
+
+        def empty_z(half, r):
+            tile = stage.tile([P, D], F32, name="z_out", bufs=4)
+            empty(("ez", half, r), tile[:], banks["z", half, r][:])
+            nc.sync.dma_start(out=(out_k, out_v)[half][r * P : (r + 1) * P, :], in_=tile[:])
+
+        def spread_gain(pair):
+            bank = psum.tile([P, 2, KP], BF16, name="bank")
+            banks["gain", pair] = bank
+            for i in range(2):
+                g = 2 * pair + i
+                src = rows[:, g * KP : (g + 1) * KP].rearrange("r (p h e) -> r h p e", h=2, e=2)
+                nc.tensor.matmul(bank[:, i, :], lhsT=ones[:, :P], rhs=src, start=True, stop=True)
+
+        def empty_gain(pair):
+            src = banks["gain", pair][:].rearrange("p i n -> p (i n)")
+            nc.scalar.copy(out=gain_all[:, 2 * pair * KP : 2 * (pair + 1) * KP], in_=src)
+
+        def spread_bias_kv():
+            bank = psum.tile([P, 8], F32, name="bank")
+            banks["bias_kv"] = bank
+            nc.tensor.matmul(bank[:], lhsT=rows[:, T + D :], rhs=pick[:], start=True, stop=True)
+
+        def empty_bias_kv():
+            nc.vector.tensor_copy(out=bias_kv[:], in_=banks["bias_kv"][:])
+
+        def spread_bias_q():
+            bank = psum.tile([P, D], BF16, name="bank")
+            banks["bias_q"] = bank
+            nc.tensor.matmul(bank[:], lhsT=ones[:, :P], rhs=rows[:, T : T + D], start=True, stop=True)
+
+        def empty_bias_q():
+            nc.scalar.copy(out=bias_q[:], in_=banks["bias_q"][:])
+
+        def warm(n):
+            if "warm" not in banks:
+                banks["warm"] = psum.tile([P, KP], F32, name="bank")
+            nc.tensor.matmul(banks["warm"][:], lhsT=ones[:, :P], rhs=ones[:], start=True, stop=True)
+
+        nc.scalar.dma_start(out=scale_all[:], in_=w_scale.rearrange("i j -> (i j)").partition_broadcast(P))
+        nc.vector.memset(ones[:], 1.0)
+        nc.vector.memset(rows[:].bitcast(I32), 0)
+        make_identity(nc, ident[:])
+        nc.gpsimd.memset(e_plane[:].rearrange("p g n -> p (g n)").bitcast(U32), 0)
+        nc.scalar.dma_start(out=rows[0:1, 0:T], in_=gain.rearrange("(o t) -> o t", o=1))
+        nc.scalar.dma_start(out=rows[0:1, T : T + D], in_=bias[0:D].rearrange("(o t) -> o t", o=1))
+        nc.scalar.dma_start(out=rows[0:8, T + D :], in_=bias[D:].rearrange("(c p) -> c p", p=P))
+        nc.vector.tensor_copy(out=pick[:], in_=ident[:, 0:8])
+        for load in LOADS:
+            if load[0] == "w":
+                load_w(load[1], load[2])
+            else:
+                load_x(*load[1:])
+        nc.sync.dma_start(out=e_codes[:].bitcast(I32), in_=e_words.rearrange("g p n -> p g n").bitcast(I32))
+        for q in range(4):
+            nc.sync.dma_start(
+                out=e_plane[32 * q : 32 * q + 4].bitcast(I32),
+                in_=e_scales[:, 4 * q : 4 * q + 4, :].rearrange("g r n -> r g n").bitcast(I32),
+            )
+
+        steps = {
+            "wd": widen, "tw": turn_w, "ew": empty_w, "qw": quant_w, "qq": quant_wq, "sx": sort_x, "tx": turn_x,
+            "ex": empty_x, "qx": quant_x, "mk": mul_kv, "ek": empty_kv, "tk": turn_kv, "et": empty_turned_kv,
+            "qk": quant_kv, "mq": mul_q, "eq": empty_q, "mz": mul_z, "ez": empty_z, "gain": spread_gain,
+            "eg": empty_gain, "bias": spread_bias_kv, "eb": empty_bias_kv, "biasq": spread_bias_q, "ebq": empty_bias_q,
+            "warm": warm,
+        }
+        for step in PLAN:
+            steps[step[0]](*step[1:])
+
+
+KV_BUFS = 20
+LOADS = [('w', 4, 2), ('x', 0, 0, 0, 2), ('w', 6, 2), ('x', 0, 0, 2, 2), ('x', 0, 1, 0, 2), ('x', 0, 1, 2, 2), ('x', 1, 0, 0, 4), ('x', 1, 1, 0, 4), ('x', 2, 0, 0, 4), ('x', 2, 1, 0, 4), ('w', 0, 4), ('x', 3, 0, 0, 4), ('x', 3, 1, 0, 4), ('w', 8, 4)]
+WIDEN_ON_VECTOR = [4, 4, 4, 4, 8, 8, 8, 8, 4, 4, 4, 4]
+EMPTY_ON_VECTOR = [('ew', 4), ('ew', 5), ('ex', 0, 0, 1), ('ex', 0, 1, 0), ('ex', 1, 1, 1)]
+PLAN = [
+    ('wd', 4),
+    ('wd', 5),
+    ('warm', 0),
+    ('wd', 6),
+    ('warm', 1),
+    ('warm', 2),
+    ('warm', 3),
+    ('warm', 4),
+    ('gain', 0),
+    ('sx', 0, 0),
+    ('eg', 0),
+    ('tw', 4),
+    ('ew', 4),
+    ('tw', 5),
+    ('ew', 5),
+    ('tw', 6),
+    ('wd', 7),
+    ('ew', 6),
+    ('gain', 1),
+    ('qw', 4),
+    ('eg', 1),
+    ('qw', 5),
+    ('tx', 1, 0, 0),
+    ('sx', 0, 1),
+    ('ex', 1, 0, 0),
+    ('qw', 6),
+    ('tx', 1, 0, 1),
+    ('ex', 1, 0, 1),
+    ('tx', 0, 0, 0),
+    ('ex', 0, 0, 0),
+    ('tx', 0, 0, 1),
+    ('ex', 0, 0, 1),
+    ('tx', 1, 1, 0),
+    ('ex', 1, 1, 0),
+    ('qx', 1, 0),
+    ('tx', 1, 1, 1),
+    ('ex', 1, 1, 1),
+    ('tw', 7),
+    ('ew', 7),
+    ('qx', 0, 0),
+    ('tx', 2, 0, 0),
+    ('ex', 2, 0, 0),
+    ('tx', 2, 0, 1),
+    ('ex', 2, 0, 1),
+    ('qx', 1, 1),
+    ('tx', 0, 1, 0),
+    ('ex', 0, 1, 0),
+    ('qw', 7),
+    ('tx', 0, 1, 1),
+    ('ex', 0, 1, 1),
+    ('tx', 2, 1, 0),
+    ('ex', 2, 1, 0),
+    ('qx', 2, 0),
+    ('tx', 2, 1, 1),
+    ('ex', 2, 1, 1),
+    ('bias',),
+    ('eb',),
+    ('qx', 0, 1),
+    ('biasq',),
+    ('ebq',),
+    ('mk', 1, 0),
+    ('qx', 2, 1),
+    ('ek', 1, 0),
+    ('mk', 1, 1),
+    ('ek', 1, 1),
+    ('mk', 1, 2),
+    ('ek', 1, 2),
+    ('mk', 1, 3),
+    ('sx', 3, 0),
+    ('ek', 1, 3),
+    ('mk', 2, 0),
+    ('wd', 0),
+    ('ek', 2, 0),
+    ('mk', 2, 1),
+    ('sx', 3, 1),
+    ('ek', 2, 1),
+    ('mk', 2, 2),
+    ('wd', 1),
+    ('wd', 2),
+    ('ek', 2, 2),
+    ('mk', 2, 3),
+    ('ek', 2, 3),
+    ('tx', 3, 0, 0),
+    ('ex', 3, 0, 0),
+    ('tx', 3, 0, 1),
+    ('ex', 3, 0, 1),
+    ('tw', 0),
+    ('ew', 0),
+    ('tx', 3, 1, 0),
+    ('ex', 3, 1, 0),
+    ('tx', 3, 1, 1),
+    ('ex', 3, 1, 1),
+    ('qx', 3, 0),
+    ('tw', 1),
+    ('ew', 1),
+    ('tw', 2),
+    ('ew', 2),
+    ('mk', 0, 0),
+    ('qx', 3, 1),
+    ('ek', 0, 0),
+    ('mk', 0, 1),
+    ('ek', 0, 1),
+    ('mk', 0, 2),
+    ('ek', 0, 2),
+    ('mk', 0, 3),
+    ('ek', 0, 3),
+    ('mk', 3, 0),
+    ('wd', 8),
+    ('ek', 3, 0),
+    ('mk', 3, 1),
+    ('wd', 9),
+    ('wd', 3),
+    ('ek', 3, 1),
+    ('mk', 3, 2),
+    ('ek', 3, 2),
+    ('mk', 3, 3),
+    ('ek', 3, 3),
+    ('tk', 1, 0),
+    ('wd', 10),
+    ('et', 1, 0),
+    ('tk', 1, 1),
+    ('wd', 11),
+    ('et', 1, 1),
+    ('tw', 8),
+    ('ew', 8),
+    ('tw', 9),
+    ('ew', 9),
+    ('qk', 1, 0),
+    ('tw', 3),
+    ('ew', 3),
+    ('tk', 0, 0),
+    ('et', 0, 0),
+    ('qw', 8),
+    ('tk', 0, 1),
+    ('et', 0, 1),
+    ('qw', 9),
+    ('tk', 3, 0),
+    ('et', 3, 0),
+    ('qq', 0),
+    ('qq', 1),
+    ('tk', 3, 1),
+    ('et', 3, 1),
+    ('qk', 0, 0),
+    ('tw', 10),
+    ('ew', 10),
+    ('tw', 11),
+    ('ew', 11),
+    ('qk', 3, 0),
+    ('tk', 2, 0),
+    ('et', 2, 0),
+    ('tk', 2, 1),
+    ('et', 2, 1),
+    ('qw', 10),
+    ('mk', 2, 4),
+    ('qw', 11),
+    ('ek', 2, 4),
+    ('qk', 2, 0),
+    ('mk', 2, 5),
+    ('ek', 2, 5),
+    ('mq', 2, 0),
+    ('eq', 2, 0),
+    ('mq', 2, 1),
+    ('eq', 2, 1),
+    ('mk', 3, 4),
+    ('ek', 3, 4),
+    ('mk', 3, 5),
+    ('ek', 3, 5),
+    ('mk', 1, 4),
+    ('ek', 1, 4),
+    ('mk', 1, 5),
+    ('ek', 1, 5),
+    ('mq', 3, 0),
+    ('eq', 3, 0),
+    ('mq', 3, 1),
+    ('eq', 3, 1),
+    ('mk', 0, 4),
+    ('ek', 0, 4),
+    ('mk', 0, 5),
+    ('ek', 0, 5),
+    ('mz', 0, 0),
+    ('ez', 0, 0),
+    ('mz', 0, 1),
+    ('ez', 0, 1),
+    ('mk', 1, 6),
+    ('ek', 1, 6),
+    ('mk', 1, 7),
+    ('ek', 1, 7),
+    ('mk', 2, 6),
+    ('ek', 2, 6),
+    ('mk', 2, 7),
+    ('ek', 2, 7),
+    ('mk', 0, 6),
+    ('ek', 0, 6),
+    ('mk', 0, 7),
+    ('ek', 0, 7),
+    ('mk', 3, 6),
+    ('ek', 3, 6),
+    ('mk', 3, 7),
+    ('ek', 3, 7),
+    ('mq', 3, 2),
+    ('eq', 3, 2),
+    ('mq', 3, 3),
+    ('eq', 3, 3),
+    ('mq', 2, 2),
+    ('eq', 2, 2),
+    ('mq', 2, 3),
+    ('eq', 2, 3),
+    ('tk', 1, 2),
+    ('et', 1, 2),
+    ('tk', 1, 3),
+    ('et', 1, 3),
+    ('tk', 0, 2),
+    ('et', 0, 2),
+    ('tk', 0, 3),
+    ('et', 0, 3),
+    ('qk', 1, 1),
+    ('tk', 2, 2),
+    ('et', 2, 2),
+    ('tk', 2, 3),
+    ('et', 2, 3),
+    ('qk', 0, 1),
+    ('tk', 3, 2),
+    ('et', 3, 2),
+    ('tk', 3, 3),
+    ('et', 3, 3),
+    ('qk', 2, 1),
+    ('mq', 1, 0),
+    ('eq', 1, 0),
+    ('qk', 3, 1),
+    ('mq', 1, 1),
+    ('eq', 1, 1),
+    ('mz', 0, 2),
+    ('ez', 0, 2),
+    ('mq', 0, 0),
+    ('eq', 0, 0),
+    ('mq', 0, 1),
+    ('eq', 0, 1),
+    ('mz', 1, 0),
+    ('ez', 1, 0),
+    ('mq', 0, 2),
+    ('eq', 0, 2),
+    ('mq', 0, 3),
+    ('eq', 0, 3),
+    ('mz', 1, 1),
+    ('ez', 1, 1),
+    ('mq', 1, 2),
+    ('eq', 1, 2),
+    ('mq', 1, 3),
+    ('eq', 1, 3),
+    ('mz', 0, 3),
+    ('ez', 0, 3),
+    ('mz', 1, 2),
+    ('ez', 1, 2),
+    ('mz', 1, 3),
+    ('ez', 1, 3),
+]

@@ -44,17 +44,16 @@ def tile_qkv_token_compression_d4_kernel(
         bias_q = keep.tile([P, D], BF16, name="bias_q")
         bias_kv = keep.tile([P, 8], F32, name="bias_kv")
         scale_all = keep.tile([P, W_TILES * BLOCKS], F32, name="scale_all")
-        e_codes = keep.tile([P, GROUPS, 2 * R], U8, name="e_codes", align_bytes=64)
-        e_plane = keep.tile([P, GROUPS, R], U8, name="e_plane", align_bytes=64)
-        x_codes = keep.tile([P, GROUPS, PASSES, KP], U32, name="x_codes", align_bytes=64)
-        x_plane = keep.tile([P, GROUPS, PASSES, KP], U8, name="x_plane", align_bytes=64)
-        wkv_codes = keep.tile([P, 8, PASSES, P], U32, name="wkv_codes", align_bytes=64)
-        wkv_plane = keep.tile([P, 8, PASSES, P], U8, name="wkv_plane", align_bytes=64)
-        wq_grouped = keep.tile([P, PASSES, D, 2], F32, name="wq_grouped", align_bytes=64)
-        wq_codes = keep.tile([P, PASSES, D], U32, name="wq_codes", align_bytes=64)
-        wq_plane = keep.tile([P, PASSES, D], U8, name="wq_plane", align_bytes=64)
-        kv_codes = keep.tile([P, GROUPS, 2, D], U32, name="kv_codes", align_bytes=64)
-        kv_plane = keep.tile([P, GROUPS, 2, D], U8, name="kv_plane", align_bytes=64)
+        e_codes = keep.tile([P, GROUPS, 2 * R], U8, name="e_codes", align_bytes=256)
+        e_plane = keep.tile([P, GROUPS, R], U8, name="e_plane", align_bytes=256)
+        x_codes = keep.tile([P, GROUPS, PASSES, KP], U32, name="x_codes", align_bytes=256)
+        x_plane = keep.tile([P, GROUPS, PASSES, KP], U8, name="x_plane", align_bytes=256)
+        wkv_codes = keep.tile([P, 8, PASSES, P], U32, name="wkv_codes", align_bytes=256)
+        wkv_plane = keep.tile([P, 8, PASSES, P], U8, name="wkv_plane", align_bytes=256)
+        wq_codes = keep.tile([P, PASSES, D], U32, name="wq_codes", align_bytes=256)
+        wq_plane = keep.tile([P, PASSES, D], U8, name="wq_plane", align_bytes=256)
+        kv_codes = keep.tile([P, GROUPS, 2, D], U32, name="kv_codes", align_bytes=256)
+        kv_plane = keep.tile([P, GROUPS, 2, D], U8, name="kv_plane", align_bytes=256)
 
         x_raw, w_raw, x_sorted, w_wide, banks, grouped, kv_rows, q_out = {}, {}, {}, {}, {}, {}, {}, {}
 
@@ -71,95 +70,94 @@ def tile_qkv_token_compression_d4_kernel(
             for i in range(count):
                 w_raw[first + i] = tile[:, i, :]
 
-        def empty(step, out, in_):
-            if step in EMPTY_ON_VECTOR:
-                nc.vector.tensor_copy(out=out, in_=in_)
+        def load_e():
+            nc.sync.dma_start(out=e_codes[:].bitcast(I32), in_=e_words.rearrange("g p n -> p g n").bitcast(I32))
+            for q in range(4):
+                nc.sync.dma_start(
+                    out=e_plane[32 * q : 32 * q + 4].bitcast(I32),
+                    in_=e_scales[:, 4 * q : 4 * q + 4, :].rearrange("g r n -> r g n").bitcast(I32),
+                )
+
+        on_vector = set(EMPTY_ON_VECTOR)
+
+        def empty(key, order):
+            tile = stage.tile([P, KP], F32, name="grouped", bufs=8, align_bytes=64)
+            grouped[key] = tile
+            src = banks[key][:].rearrange(order)
+            dst = tile[:].rearrange("p (a b c) -> p a b c", a=src.shape[1], b=src.shape[2])
+            if key in on_vector:
+                nc.vector.tensor_copy(out=dst, in_=src)
             else:
-                nc.scalar.copy(out=out, in_=in_)
+                nc.scalar.copy(out=dst, in_=src)
+
+        def quantise(codes, plane, words):
+            nc.vector.quantize_mx(out=codes.bitcast(FP8X4), scales=plane, in_=words.bitcast(BF16))
 
         def widen(i):
-            on_vector = WIDEN_ON_VECTOR[i]
             wide = stage.tile([P, C], BF16, name="w_wide", bufs=6)
             w_wide[i] = wide
             for j in range(BLOCKS):
                 cols = slice(j * P, (j + 1) * P)
                 scale = scale_all[:, i * BLOCKS + j : i * BLOCKS + j + 1]
-                if j < on_vector:
-                    k, b = divmod(j, 4)
-                    dst = wide[:, k * KP : (k + 1) * KP].rearrange("p (u q e) -> p q u e", u=2, e=2)
-                    nc.vector.tensor_scalar(
-                        out=dst[:, 32 * b : 32 * (b + 1)],
-                        in0=w_raw[i][:, cols].bitcast(FP8).rearrange("p (q u e) -> p q u e", u=2, e=2),
-                        scalar1=scale,
-                        scalar2=None,
-                        op0=MULT,
-                    )
+                src = w_raw[i][:, cols].bitcast(FP8)
+                if j < WIDEN_ON_VECTOR[i // 4]:
+                    nc.vector.tensor_scalar(out=wide[:, cols], in0=src, scalar1=scale, scalar2=None, op0=MULT)
                 else:
-                    nc.scalar.activation(out=wide[:, cols], in_=w_raw[i][:, cols].bitcast(FP8), func=COPY, scale=scale)
+                    nc.scalar.activation(out=wide[:, cols], in_=src, func=COPY, scale=scale)
+
+        def sort_w(i):
+            tile = stage.tile([P, 2, 2, P], F32, name="x_sorted", bufs=6)
+            x_sorted["w", i] = tile
+            nc.scalar.copy(out=tile[:], in_=w_wide[i][:].bitcast(F32).rearrange("p (k q u) -> p k u q", k=2, u=2))
 
         def turn_w(i):
             bank = psum.tile([P, PASSES, 2, P], F32, name="bank")
-            banks["w", i] = bank
+            banks["tw", i] = bank
             words = w_wide[i][:].bitcast(F32)
             for k in range(PASSES):
                 for u in range(2):
-                    if 4 * k < WIDEN_ON_VECTOR[i]:
-                        src = words[:, 256 * k + P * u : 256 * k + P * (u + 1)]
+                    if ("w", i) in x_sorted:
+                        src = x_sorted["w", i][:, k, u, :]
                     else:
                         src = words[:, 256 * k + u : 256 * (k + 1) : 2]
                     nc.tensor.transpose(bank[:, k, u, :], src, ident[:])
 
         def empty_w(i):
-            src = banks["w", i][:].rearrange("p k u n -> p k n u")
-            if i < 4:
-                empty(("ew", i), wq_grouped[:, :, i * P : (i + 1) * P, :], src)
-            else:
-                tile = stage.tile([P, PASSES, P, 2], F32, name="w_grouped", align_bytes=64)
-                grouped["w", i] = tile
-                empty(("ew", i), tile[:], src)
+            empty(("tw", i), "p k u n -> p k n u")
 
         def quant_w(i):
-            nc.vector.quantize_mx(
-                out=wkv_codes[:, i - 4].rearrange("p k n -> p (k n)").bitcast(FP8X4),
-                scales=wkv_plane[:, i - 4].rearrange("p k n -> p (k n)"),
-                in_=grouped["w", i][:].rearrange("p k n u -> p (k n u)").bitcast(BF16),
-            )
+            words = grouped["tw", i]
+            if i >= 4:
+                codes = wkv_codes[:, i - 4].rearrange("p k n -> p (k n)")
+                quantise(codes, wkv_plane[:, i - 4].rearrange("p k n -> p (k n)"), words[:])
+            else:
+                cols = slice(i * P, (i + 1) * P)
+                for k in range(PASSES):
+                    quantise(wq_codes[:, k, cols], wq_plane[:, k, cols], words[:, 256 * k : 256 * (k + 1)])
 
-        def quant_wq(k):
-            nc.vector.quantize_mx(
-                out=wq_codes[:, k, :].bitcast(FP8X4),
-                scales=wq_plane[:, k, :],
-                in_=wq_grouped[:, k].rearrange("p n u -> p (n u)").bitcast(BF16),
-            )
-
-        def sort_x(g, k):
-            tile = stage.tile([P, 4, 2, P], F32, name="x_sorted")
-            x_sorted[g, k] = tile
-            words = x_raw[g, k][:].rearrange("p t c -> p (t c)").bitcast(F32)
-            nc.scalar.copy(out=tile[:], in_=words.rearrange("p (t q u) -> p t u q", t=4, u=2))
+        def sort_x(g, k, h):
+            tile = stage.tile([P, 2, 2, P], F32, name="x_sorted", bufs=6)
+            x_sorted[g, k, h] = tile
+            words = x_raw[g, k][:, 2 * h : 2 * h + 2, :].rearrange("p e c -> p (e c)").bitcast(F32)
+            nc.scalar.copy(out=tile[:], in_=words.rearrange("p (e q u) -> p e u q", e=2, u=2))
 
         def turn_x(g, k, h):
             bank = psum.tile([P, 2, 2, P], F32, name="bank")
-            banks["x", g, k, h] = bank
+            banks["tx", g, k, h] = bank
             for e in range(2):
                 for u in range(2):
-                    if (g, k) in x_sorted:
-                        src = x_sorted[g, k][:, 2 * h + e, u, :]
+                    if g in SORTED_GROUPS:
+                        src = x_sorted[g, k, h][:, e, u, :]
                     else:
                         src = x_raw[g, k][:, 2 * h + e, :].bitcast(F32)[:, u:256:2]
                     nc.tensor.transpose(bank[:, e, u, :], src, ident[:])
 
         def empty_x(g, k, h):
-            if ("x", g, k) not in grouped:
-                grouped["x", g, k] = stage.tile([P, 2, P, 4], F32, name="grouped", bufs=4, align_bytes=64)
-            empty(("ex", g, k, h), grouped["x", g, k][:, h], banks["x", g, k, h][:].rearrange("q e u p -> q p (e u)"))
+            empty(("tx", g, k, h), "q e u p -> q p e u")
 
-        def quant_x(g, k):
-            nc.vector.quantize_mx(
-                out=x_codes[:, g, k, :].bitcast(FP8X4),
-                scales=x_plane[:, g, k, :],
-                in_=grouped["x", g, k][:].rearrange("q h p w -> q (h p w)").bitcast(BF16),
-            )
+        def quant_x(g, k, h):
+            cols = slice(256 * h, 256 * (h + 1))
+            quantise(x_codes[:, g, k, cols], x_plane[:, g, k, cols], grouped["tx", g, k, h][:])
 
         def mul_kv(g, c):
             bank = psum.tile([P, KP], F32, name="bank")
@@ -189,24 +187,19 @@ def tile_qkv_token_compression_d4_kernel(
 
         def turn_kv(g, pair):
             bank = psum.tile([P, 2, 2, P], F32, name="bank")
-            banks["t", g, pair] = bank
+            banks["tk", g, pair] = bank
             for i in range(2):
                 words = kv_rows[g, 2 * pair + i][:].bitcast(F32)
                 for h in range(2):
                     nc.tensor.transpose(bank[:, i, h, :], words[:, h * P : (h + 1) * P], ident[:])
 
         def empty_turned_kv(g, pair):
-            if ("kv", g, pair // 2) not in grouped:
-                grouped["kv", g, pair // 2] = stage.tile([P, 4, P, 2], F32, name="grouped", bufs=4, align_bytes=64)
-            lo = 2 * (pair % 2)
-            empty(("et", g, pair), grouped["kv", g, pair // 2][:, lo : lo + 2], banks["t", g, pair][:].rearrange("p i h n -> p i n h"))
+            empty(("tk", g, pair), "p i h n -> p i n h")
 
-        def quant_kv(g, half):
-            nc.vector.quantize_mx(
-                out=kv_codes[:, g, half, :].bitcast(FP8X4),
-                scales=kv_plane[:, g, half, :],
-                in_=grouped["kv", g, half][:].rearrange("p i n h -> p (i n h)").bitcast(BF16),
-            )
+        def quant_kv(g, pair):
+            half, lo = divmod(pair, 2)
+            cols = slice(256 * lo, 256 * (lo + 1))
+            quantise(kv_codes[:, g, half, cols], kv_plane[:, g, half, cols], grouped["tk", g, pair][:])
 
         def mul_q(g, j):
             bank = psum.tile([P, D], F32, name="bank")
@@ -249,20 +242,17 @@ def tile_qkv_token_compression_d4_kernel(
 
         def empty_z(half, r):
             tile = stage.tile([P, D], F32, name="z_out", bufs=4)
-            empty(("ez", half, r), tile[:], banks["z", half, r][:])
+            nc.scalar.copy(out=tile[:], in_=banks["z", half, r][:])
             nc.sync.dma_start(out=(out_k, out_v)[half][r * P : (r + 1) * P, :], in_=tile[:])
 
-        def spread_gain(pair):
-            bank = psum.tile([P, 2, KP], BF16, name="bank")
-            banks["gain", pair] = bank
-            for i in range(2):
-                g = 2 * pair + i
-                src = rows[:, g * KP : (g + 1) * KP].rearrange("r (p h e) -> r h p e", h=2, e=2)
-                nc.tensor.matmul(bank[:, i, :], lhsT=ones[:, :P], rhs=src, start=True, stop=True)
+        def spread_gain(g):
+            bank = psum.tile([P, KP], BF16, name="bank")
+            banks["gain", g] = bank
+            src = rows[:, g * KP : (g + 1) * KP].rearrange("r (p h e) -> r h p e", h=2, e=2)
+            nc.tensor.matmul(bank[:], lhsT=ones[:, :P], rhs=src, start=True, stop=True)
 
-        def empty_gain(pair):
-            src = banks["gain", pair][:].rearrange("p i n -> p (i n)")
-            nc.scalar.copy(out=gain_all[:, 2 * pair * KP : 2 * (pair + 1) * KP], in_=src)
+        def empty_gain(g):
+            nc.scalar.copy(out=gain_all[:, g * KP : (g + 1) * KP], in_=banks["gain", g][:])
 
         def spread_bias_kv():
             bank = psum.tile([P, 8], F32, name="bank")
@@ -281,9 +271,8 @@ def tile_qkv_token_compression_d4_kernel(
             nc.scalar.copy(out=bias_q[:], in_=banks["bias_q"][:])
 
         def warm(n):
-            if "warm" not in banks:
-                banks["warm"] = psum.tile([P, KP], F32, name="bank")
-            nc.tensor.matmul(banks["warm"][:], lhsT=ones[:, :P], rhs=ones[:], start=True, stop=True)
+            bank = psum.tile([P, KP], F32, name="bank")
+            nc.tensor.matmul(bank[:], lhsT=ones[:, :P], rhs=ones[:], start=True, stop=True)
 
         nc.scalar.dma_start(out=scale_all[:], in_=w_scale.rearrange("i j -> (i j)").partition_broadcast(P))
         nc.vector.memset(ones[:], 1.0)
@@ -293,21 +282,17 @@ def tile_qkv_token_compression_d4_kernel(
         nc.scalar.dma_start(out=rows[0:1, 0:T], in_=gain.rearrange("(o t) -> o t", o=1))
         nc.scalar.dma_start(out=rows[0:1, T : T + D], in_=bias[0:D].rearrange("(o t) -> o t", o=1))
         nc.scalar.dma_start(out=rows[0:8, T + D :], in_=bias[D:].rearrange("(c p) -> c p", p=P))
-        nc.vector.tensor_copy(out=pick[:], in_=ident[:, 0:8])
+        nc.scalar.copy(out=pick[:], in_=ident[:, 0:8])
         for load in LOADS:
             if load[0] == "w":
                 load_w(load[1], load[2])
-            else:
+            elif load[0] == "x":
                 load_x(*load[1:])
-        nc.sync.dma_start(out=e_codes[:].bitcast(I32), in_=e_words.rearrange("g p n -> p g n").bitcast(I32))
-        for q in range(4):
-            nc.sync.dma_start(
-                out=e_plane[32 * q : 32 * q + 4].bitcast(I32),
-                in_=e_scales[:, 4 * q : 4 * q + 4, :].rearrange("g r n -> r g n").bitcast(I32),
-            )
+            else:
+                load_e()
 
         steps = {
-            "wd": widen, "tw": turn_w, "ew": empty_w, "qw": quant_w, "qq": quant_wq, "sx": sort_x, "tx": turn_x,
+            "wd": widen, "tw": turn_w, "ew": empty_w, "qw": quant_w, "sx": sort_x, "sw": sort_w, "tx": turn_x,
             "ex": empty_x, "qx": quant_x, "mk": mul_kv, "ek": empty_kv, "tk": turn_kv, "et": empty_turned_kv,
             "qk": quant_kv, "mq": mul_q, "eq": empty_q, "mz": mul_z, "ez": empty_z, "gain": spread_gain,
             "eg": empty_gain, "bias": spread_bias_kv, "eb": empty_bias_kv, "biasq": spread_bias_q, "ebq": empty_bias_q,
@@ -318,213 +303,260 @@ def tile_qkv_token_compression_d4_kernel(
 
 
 KV_BUFS = 20
-LOADS = [('w', 4, 2), ('x', 0, 0, 0, 2), ('w', 6, 2), ('x', 0, 0, 2, 2), ('x', 0, 1, 0, 2), ('x', 0, 1, 2, 2), ('x', 1, 0, 0, 4), ('x', 1, 1, 0, 4), ('x', 2, 0, 0, 4), ('x', 2, 1, 0, 4), ('w', 0, 4), ('x', 3, 0, 0, 4), ('x', 3, 1, 0, 4), ('w', 8, 4)]
-WIDEN_ON_VECTOR = [4, 4, 4, 4, 8, 8, 8, 8, 4, 4, 4, 4]
-EMPTY_ON_VECTOR = [('ew', 4), ('ew', 5), ('ex', 0, 0, 1), ('ex', 0, 1, 0), ('ex', 1, 1, 1)]
+LOADS = [('w', 4, 2), ('x', 0, 0, 0, 2), ('x', 0, 0, 2, 2), ('x', 0, 1, 0, 2), ('x', 0, 1, 2, 2), ('w', 6, 2), ('x', 1, 0, 0, 4), ('x', 1, 1, 0, 4), ('x', 2, 0, 0, 4), ('x', 2, 1, 0, 4), ('w', 8, 4), ('x', 3, 0, 0, 4), ('x', 3, 1, 0, 4), ('w', 0, 4), ('e',)]
+WIDEN_ON_VECTOR = [3, 7, 8]
+SORTED_GROUPS = [0, 1, 2, 3]
+EMPTY_ON_VECTOR = [('tw', 4), ('tw', 6), ('tx', 0, 0, 1), ('tx', 0, 1, 1), ('tx', 1, 0, 0), ('tx', 1, 1, 0)]
 PLAN = [
     ('wd', 4),
-    ('wd', 5),
+    ('sx', 0, 0, 0),
+    ('sx', 0, 0, 1),
+    ('sx', 0, 1, 0),
     ('warm', 0),
-    ('wd', 6),
+    ('sx', 0, 1, 1),
+    ('wd', 5),
     ('warm', 1),
     ('warm', 2),
-    ('warm', 3),
-    ('warm', 4),
     ('gain', 0),
-    ('sx', 0, 0),
     ('eg', 0),
+    ('wd', 6),
     ('tw', 4),
     ('ew', 4),
-    ('tw', 5),
-    ('ew', 5),
-    ('tw', 6),
     ('wd', 7),
-    ('ew', 6),
-    ('gain', 1),
+    ('biasq',),
+    ('ebq',),
+    ('bias',),
+    ('eb',),
     ('qw', 4),
-    ('eg', 1),
-    ('qw', 5),
-    ('tx', 1, 0, 0),
-    ('sx', 0, 1),
-    ('ex', 1, 0, 0),
-    ('qw', 6),
-    ('tx', 1, 0, 1),
-    ('ex', 1, 0, 1),
     ('tx', 0, 0, 0),
     ('ex', 0, 0, 0),
     ('tx', 0, 0, 1),
     ('ex', 0, 0, 1),
-    ('tx', 1, 1, 0),
-    ('ex', 1, 1, 0),
-    ('qx', 1, 0),
-    ('tx', 1, 1, 1),
-    ('ex', 1, 1, 1),
+    ('tx', 0, 1, 0),
+    ('ex', 0, 1, 0),
+    ('qx', 0, 0, 0),
+    ('tx', 0, 1, 1),
+    ('ex', 0, 1, 1),
+    ('sx', 1, 0, 0),
+    ('qx', 0, 0, 1),
+    ('tw', 5),
+    ('ew', 5),
+    ('sx', 1, 0, 1),
+    ('qx', 0, 1, 0),
+    ('gain', 1),
+    ('eg', 1),
+    ('sx', 1, 1, 0),
+    ('qx', 0, 1, 1),
+    ('gain', 2),
+    ('eg', 2),
+    ('sx', 1, 1, 1),
+    ('qw', 5),
+    ('tw', 6),
+    ('ew', 6),
     ('tw', 7),
     ('ew', 7),
-    ('qx', 0, 0),
+    ('mk', 0, 0),
+    ('ek', 0, 0),
+    ('qw', 6),
+    ('qw', 7),
+    ('mk', 0, 1),
+    ('ek', 0, 1),
+    ('sx', 2, 0, 0),
+    ('tx', 1, 0, 0),
+    ('ex', 1, 0, 0),
+    ('sx', 2, 0, 1),
+    ('tx', 1, 0, 1),
+    ('ex', 1, 0, 1),
+    ('sx', 2, 1, 0),
+    ('tx', 1, 1, 0),
+    ('ex', 1, 1, 0),
+    ('sx', 2, 1, 1),
+    ('wd', 8),
+    ('qx', 1, 0, 0),
+    ('tx', 1, 1, 1),
+    ('ex', 1, 1, 1),
+    ('qx', 1, 0, 1),
+    ('gain', 3),
+    ('eg', 3),
+    ('qx', 1, 1, 0),
+    ('mk', 0, 2),
+    ('ek', 0, 2),
+    ('qx', 1, 1, 1),
+    ('mk', 0, 3),
+    ('ek', 0, 3),
     ('tx', 2, 0, 0),
     ('ex', 2, 0, 0),
     ('tx', 2, 0, 1),
     ('ex', 2, 0, 1),
-    ('qx', 1, 1),
-    ('tx', 0, 1, 0),
-    ('ex', 0, 1, 0),
-    ('qw', 7),
-    ('tx', 0, 1, 1),
-    ('ex', 0, 1, 1),
     ('tx', 2, 1, 0),
     ('ex', 2, 1, 0),
-    ('qx', 2, 0),
+    ('wd', 9),
+    ('qx', 2, 0, 0),
     ('tx', 2, 1, 1),
     ('ex', 2, 1, 1),
-    ('bias',),
-    ('eb',),
-    ('qx', 0, 1),
-    ('biasq',),
-    ('ebq',),
+    ('qx', 2, 0, 1),
+    ('tw', 8),
+    ('ew', 8),
+    ('sx', 3, 0, 0),
+    ('qx', 2, 1, 0),
     ('mk', 1, 0),
-    ('qx', 2, 1),
     ('ek', 1, 0),
+    ('sx', 3, 0, 1),
+    ('qx', 2, 1, 1),
+    ('qw', 8),
     ('mk', 1, 1),
     ('ek', 1, 1),
+    ('sx', 3, 1, 0),
     ('mk', 1, 2),
     ('ek', 1, 2),
+    ('sx', 3, 1, 1),
     ('mk', 1, 3),
-    ('sx', 3, 0),
     ('ek', 1, 3),
-    ('mk', 2, 0),
-    ('wd', 0),
-    ('ek', 2, 0),
-    ('mk', 2, 1),
-    ('sx', 3, 1),
-    ('ek', 2, 1),
-    ('mk', 2, 2),
-    ('wd', 1),
-    ('wd', 2),
-    ('ek', 2, 2),
-    ('mk', 2, 3),
-    ('ek', 2, 3),
+    ('tw', 9),
+    ('ew', 9),
     ('tx', 3, 0, 0),
     ('ex', 3, 0, 0),
     ('tx', 3, 0, 1),
     ('ex', 3, 0, 1),
-    ('tw', 0),
-    ('ew', 0),
+    ('qw', 9),
+    ('mk', 2, 0),
+    ('ek', 2, 0),
+    ('qx', 3, 0, 0),
+    ('qx', 3, 0, 1),
     ('tx', 3, 1, 0),
     ('ex', 3, 1, 0),
     ('tx', 3, 1, 1),
     ('ex', 3, 1, 1),
-    ('qx', 3, 0),
-    ('tw', 1),
-    ('ew', 1),
-    ('tw', 2),
-    ('ew', 2),
-    ('mk', 0, 0),
-    ('qx', 3, 1),
-    ('ek', 0, 0),
-    ('mk', 0, 1),
-    ('ek', 0, 1),
-    ('mk', 0, 2),
-    ('ek', 0, 2),
-    ('mk', 0, 3),
-    ('ek', 0, 3),
-    ('mk', 3, 0),
-    ('wd', 8),
-    ('ek', 3, 0),
-    ('mk', 3, 1),
-    ('wd', 9),
-    ('wd', 3),
-    ('ek', 3, 1),
-    ('mk', 3, 2),
-    ('ek', 3, 2),
-    ('mk', 3, 3),
-    ('ek', 3, 3),
-    ('tk', 1, 0),
-    ('wd', 10),
-    ('et', 1, 0),
-    ('tk', 1, 1),
-    ('wd', 11),
-    ('et', 1, 1),
-    ('tw', 8),
-    ('ew', 8),
-    ('tw', 9),
-    ('ew', 9),
-    ('qk', 1, 0),
-    ('tw', 3),
-    ('ew', 3),
     ('tk', 0, 0),
     ('et', 0, 0),
-    ('qw', 8),
+    ('qx', 3, 1, 0),
     ('tk', 0, 1),
     ('et', 0, 1),
-    ('qw', 9),
-    ('tk', 3, 0),
-    ('et', 3, 0),
-    ('qq', 0),
-    ('qq', 1),
-    ('tk', 3, 1),
-    ('et', 3, 1),
+    ('qx', 3, 1, 1),
+    ('mk', 2, 1),
+    ('ek', 2, 1),
     ('qk', 0, 0),
+    ('wd', 0),
+    ('qk', 0, 1),
+    ('mk', 2, 2),
+    ('ek', 2, 2),
+    ('wd', 1),
+    ('wd', 10),
+    ('mk', 2, 3),
+    ('ek', 2, 3),
+    ('mk', 3, 0),
+    ('ek', 3, 0),
+    ('mk', 3, 1),
+    ('ek', 3, 1),
+    ('tk', 1, 0),
+    ('et', 1, 0),
+    ('wd', 11),
+    ('tk', 1, 1),
+    ('et', 1, 1),
+    ('wd', 2),
+    ('tw', 0),
+    ('ew', 0),
+    ('wd', 3),
+    ('qk', 1, 0),
+    ('tw', 1),
+    ('ew', 1),
+    ('qk', 1, 1),
     ('tw', 10),
     ('ew', 10),
+    ('qw', 0),
+    ('mk', 3, 2),
+    ('ek', 3, 2),
+    ('qw', 1),
+    ('qw', 10),
+    ('mk', 3, 3),
+    ('ek', 3, 3),
+    ('mk', 2, 4),
+    ('ek', 2, 4),
     ('tw', 11),
     ('ew', 11),
-    ('qk', 3, 0),
+    ('tw', 2),
+    ('ew', 2),
+    ('tw', 3),
+    ('ew', 3),
+    ('qw', 11),
     ('tk', 2, 0),
     ('et', 2, 0),
+    ('qw', 2),
     ('tk', 2, 1),
     ('et', 2, 1),
-    ('qw', 10),
-    ('mk', 2, 4),
-    ('qw', 11),
-    ('ek', 2, 4),
-    ('qk', 2, 0),
+    ('qw', 3),
     ('mk', 2, 5),
     ('ek', 2, 5),
-    ('mq', 2, 0),
-    ('eq', 2, 0),
-    ('mq', 2, 1),
-    ('eq', 2, 1),
+    ('qk', 2, 0),
+    ('qk', 2, 1),
+    ('mk', 2, 6),
+    ('ek', 2, 6),
     ('mk', 3, 4),
     ('ek', 3, 4),
     ('mk', 3, 5),
     ('ek', 3, 5),
-    ('mk', 1, 4),
-    ('ek', 1, 4),
-    ('mk', 1, 5),
-    ('ek', 1, 5),
+    ('tk', 3, 0),
+    ('et', 3, 0),
+    ('tk', 3, 1),
+    ('et', 3, 1),
     ('mq', 3, 0),
     ('eq', 3, 0),
+    ('qk', 3, 0),
+    ('qk', 3, 1),
     ('mq', 3, 1),
     ('eq', 3, 1),
-    ('mk', 0, 4),
-    ('ek', 0, 4),
-    ('mk', 0, 5),
-    ('ek', 0, 5),
-    ('mz', 0, 0),
-    ('ez', 0, 0),
-    ('mz', 0, 1),
-    ('ez', 0, 1),
-    ('mk', 1, 6),
-    ('ek', 1, 6),
-    ('mk', 1, 7),
-    ('ek', 1, 7),
-    ('mk', 2, 6),
-    ('ek', 2, 6),
-    ('mk', 2, 7),
-    ('ek', 2, 7),
-    ('mk', 0, 6),
-    ('ek', 0, 6),
-    ('mk', 0, 7),
-    ('ek', 0, 7),
+    ('mq', 1, 0),
+    ('eq', 1, 0),
+    ('mq', 1, 1),
+    ('eq', 1, 1),
+    ('mq', 1, 2),
+    ('eq', 1, 2),
+    ('mq', 1, 3),
+    ('eq', 1, 3),
     ('mk', 3, 6),
     ('ek', 3, 6),
     ('mk', 3, 7),
     ('ek', 3, 7),
-    ('mq', 3, 2),
-    ('eq', 3, 2),
-    ('mq', 3, 3),
-    ('eq', 3, 3),
+    ('mk', 1, 4),
+    ('ek', 1, 4),
+    ('mk', 1, 5),
+    ('ek', 1, 5),
+    ('mk', 1, 6),
+    ('ek', 1, 6),
+    ('mk', 1, 7),
+    ('ek', 1, 7),
+    ('mk', 2, 7),
+    ('ek', 2, 7),
+    ('mq', 0, 0),
+    ('eq', 0, 0),
+    ('mq', 0, 1),
+    ('eq', 0, 1),
+    ('mk', 0, 4),
+    ('ek', 0, 4),
+    ('mk', 0, 5),
+    ('ek', 0, 5),
+    ('mk', 0, 6),
+    ('ek', 0, 6),
+    ('mk', 0, 7),
+    ('ek', 0, 7),
+    ('mz', 0, 0),
+    ('ez', 0, 0),
+    ('tk', 2, 2),
+    ('et', 2, 2),
+    ('tk', 2, 3),
+    ('et', 2, 3),
+    ('tk', 0, 2),
+    ('et', 0, 2),
+    ('qk', 2, 2),
+    ('tk', 0, 3),
+    ('et', 0, 3),
+    ('qk', 2, 3),
+    ('mq', 2, 0),
+    ('eq', 2, 0),
+    ('qk', 0, 2),
+    ('qk', 0, 3),
+    ('mq', 2, 1),
+    ('eq', 2, 1),
     ('mq', 2, 2),
     ('eq', 2, 2),
     ('mq', 2, 3),
@@ -533,46 +565,32 @@ PLAN = [
     ('et', 1, 2),
     ('tk', 1, 3),
     ('et', 1, 3),
-    ('tk', 0, 2),
-    ('et', 0, 2),
-    ('tk', 0, 3),
-    ('et', 0, 3),
-    ('qk', 1, 1),
-    ('tk', 2, 2),
-    ('et', 2, 2),
-    ('tk', 2, 3),
-    ('et', 2, 3),
-    ('qk', 0, 1),
     ('tk', 3, 2),
     ('et', 3, 2),
+    ('qk', 1, 2),
     ('tk', 3, 3),
     ('et', 3, 3),
-    ('qk', 2, 1),
-    ('mq', 1, 0),
-    ('eq', 1, 0),
-    ('qk', 3, 1),
-    ('mq', 1, 1),
-    ('eq', 1, 1),
-    ('mz', 0, 2),
-    ('ez', 0, 2),
-    ('mq', 0, 0),
-    ('eq', 0, 0),
-    ('mq', 0, 1),
-    ('eq', 0, 1),
-    ('mz', 1, 0),
-    ('ez', 1, 0),
+    ('qk', 1, 3),
+    ('mq', 3, 2),
+    ('eq', 3, 2),
+    ('qk', 3, 2),
+    ('qk', 3, 3),
+    ('mq', 3, 3),
+    ('eq', 3, 3),
     ('mq', 0, 2),
     ('eq', 0, 2),
     ('mq', 0, 3),
     ('eq', 0, 3),
-    ('mz', 1, 1),
-    ('ez', 1, 1),
-    ('mq', 1, 2),
-    ('eq', 1, 2),
-    ('mq', 1, 3),
-    ('eq', 1, 3),
+    ('mz', 0, 1),
+    ('ez', 0, 1),
+    ('mz', 0, 2),
+    ('ez', 0, 2),
     ('mz', 0, 3),
     ('ez', 0, 3),
+    ('mz', 1, 0),
+    ('ez', 1, 0),
+    ('mz', 1, 1),
+    ('ez', 1, 1),
     ('mz', 1, 2),
     ('ez', 1, 2),
     ('mz', 1, 3),

@@ -24,6 +24,7 @@ GROUPS = T // KP
 PASSES = C // KP
 W_TILES = 3 * D // P
 BLOCKS = C // P
+TG = 2 * KP
 
 
 def tile_qkv_token_compression_d4_kernel(
@@ -39,8 +40,8 @@ def tile_qkv_token_compression_d4_kernel(
         ident = keep.tile([P, P], F32, name="ident")
         pick = keep.tile([P, 8], BF16, name="pick")
         ones = keep.tile([P, KP], BF16, name="ones")
-        rows = keep.tile([P, T + D + P], BF16, name="rows")
-        gain_all = keep.tile([P, T], BF16, name="gain_all")
+        rows = keep.tile([P, TG + 3 * D + P], BF16, name="rows")
+        gain_all = keep.tile([P, TG], BF16, name="gain_all")
         bias_q = keep.tile([P, D], BF16, name="bias_q")
         bias_kv = keep.tile([P, 8], F32, name="bias_kv")
         scale_all = keep.tile([P, W_TILES * BLOCKS], F32, name="scale_all")
@@ -48,14 +49,15 @@ def tile_qkv_token_compression_d4_kernel(
         e_plane = keep.tile([P, GROUPS, R], U8, name="e_plane", align_bytes=256)
         x_codes = keep.tile([P, GROUPS, PASSES, KP], U32, name="x_codes", align_bytes=256)
         x_plane = keep.tile([P, GROUPS, PASSES, KP], U8, name="x_plane", align_bytes=256)
-        wkv_codes = keep.tile([P, 8, PASSES, P], U32, name="wkv_codes", align_bytes=256)
-        wkv_plane = keep.tile([P, 8, PASSES, P], U8, name="wkv_plane", align_bytes=256)
-        wq_codes = keep.tile([P, PASSES, D], U32, name="wq_codes", align_bytes=256)
-        wq_plane = keep.tile([P, PASSES, D], U8, name="wq_plane", align_bytes=256)
+        w_codes = keep.tile([P, 3, PASSES, D], U32, name="w_codes", align_bytes=256)
+        w_plane = keep.tile([P, 3, PASSES, D], U8, name="w_plane", align_bytes=256)
+        bias_row = keep.tile([P, 2, D], BF16, name="bias_row")
+        gain_raw = keep.tile([P, 2, 4], BF16, name="gain_raw")
+        gain_col = keep.tile([P, 2, 4], F32, name="gain_col")
         kv_codes = keep.tile([P, GROUPS, 2, D], U32, name="kv_codes", align_bytes=256)
         kv_plane = keep.tile([P, GROUPS, 2, D], U8, name="kv_plane", align_bytes=256)
 
-        x_raw, w_raw, x_sorted, w_wide, banks, grouped, kv_rows, q_out = {}, {}, {}, {}, {}, {}, {}, {}
+        x_raw, w_raw, x_sorted, w_wide, banks, grouped, kv_rows, q_out, planes = {}, {}, {}, {}, {}, {}, {}, {}, {}
 
         def load_x(g, k, first, count):
             if (g, k) not in x_raw:
@@ -71,6 +73,7 @@ def tile_qkv_token_compression_d4_kernel(
                 w_raw[first + i] = tile[:, i, :]
 
         def load_e():
+            nc.sync.dma_start(out=gain_raw[:], in_=gain[TG:].rearrange("(g p t) -> p g t", p=P, t=4))
             nc.sync.dma_start(out=e_codes[:].bitcast(I32), in_=e_words.rearrange("g p n -> p g n").bitcast(I32))
             for q in range(4):
                 nc.sync.dma_start(
@@ -126,14 +129,11 @@ def tile_qkv_token_compression_d4_kernel(
             empty(("tw", i), "p k u n -> p k n u")
 
         def quant_w(i):
-            words = grouped["tw", i]
-            if i >= 4:
-                codes = wkv_codes[:, i - 4].rearrange("p k n -> p (k n)")
-                quantise(codes, wkv_plane[:, i - 4].rearrange("p k n -> p (k n)"), words[:])
-            else:
-                cols = slice(i * P, (i + 1) * P)
-                for k in range(PASSES):
-                    quantise(wq_codes[:, k, cols], wq_plane[:, k, cols], words[:, 256 * k : 256 * (k + 1)])
+            part, lo = divmod(i, 4)
+            cols = slice(lo * P, (lo + 1) * P)
+            for k in range(PASSES):
+                words = grouped["tw", i][:, 256 * k : 256 * (k + 1)]
+                quantise(w_codes[:, part, k, cols], w_plane[:, part, k, cols], words)
 
         def sort_x(g, k, h):
             tile = stage.tile([P, 2, 2, P], F32, name="x_sorted", bufs=6)
@@ -153,27 +153,60 @@ def tile_qkv_token_compression_d4_kernel(
                     nc.tensor.transpose(bank[:, e, u, :], src, ident[:])
 
         def empty_x(g, k, h):
-            empty(("tx", g, k, h), "q e u p -> q p e u")
+            empty(("tx", g, k, h), "q e u p -> q e p u" if g in DIRECT else "q e u p -> q p e u")
 
         def quant_x(g, k, h):
             cols = slice(256 * h, 256 * (h + 1))
             quantise(x_codes[:, g, k, cols], x_plane[:, g, k, cols], grouped["tx", g, k, h][:])
 
+        def product(bank, lhs, rhs):
+            for k, ((a, a_plane), (b, b_plane)) in enumerate(zip(lhs, rhs)):
+                nc.tensor.matmul_mx(
+                    out=bank[:],
+                    lhsT=a,
+                    lhsT_scale=a_plane,
+                    rhs=b,
+                    rhs_scale=b_plane,
+                    start=(k == 0),
+                    stop=(k == len(lhs) - 1),
+                )
+
+        def x_operand(g, cols):
+            return [(x_codes[:, g, k, cols].bitcast(FP8X4), x_plane[:, g, k, cols]) for k in range(PASSES)]
+
+        def w_operand(part, cols):
+            return [(w_codes[:, part, k, cols].bitcast(FP8X4), w_plane[:, part, k, cols]) for k in range(PASSES)]
+
         def mul_kv(g, c):
             bank = psum.tile([P, KP], F32, name="bank")
             banks["kv", g, c] = bank
-            for k in range(PASSES):
-                nc.tensor.matmul_mx(
-                    out=bank[:],
-                    lhsT=wkv_codes[:, c, k, :].bitcast(FP8X4),
-                    lhsT_scale=wkv_plane[:, c, k, :],
-                    rhs=x_codes[:, g, k, :].bitcast(FP8X4),
-                    rhs_scale=x_plane[:, g, k, :],
-                    start=(k == 0),
-                    stop=(k == PASSES - 1),
-                )
+            half, i = divmod(c, 4)
+            cols = slice(i * P, (i + 1) * P)
+            if g in DIRECT:
+                product(bank, x_operand(g, cols), w_operand(1 + half, slice(0, D)))
+            else:
+                product(bank, w_operand(1 + half, cols), x_operand(g, slice(0, KP)))
+
+        def bias_gain(g, c):
+            half, t = divmod(c, 4)
+            tile = stage.tile([P, D], F32, name="bias_gain", bufs=6)
+            banks["bg", g, c] = tile
+            nc.scalar.activation(out=tile[:], in_=bias_row[:, half, :], func=COPY, scale=gain_col[:, g - 2, t : t + 1])
 
         def empty_kv(g, c):
+            if g in DIRECT:
+                half, t = divmod(c, 4)
+                if (g, half) not in planes:
+                    planes[g, half] = stage.tile([P, 4, D], BF16, name="planes", bufs=3)
+                nc.vector.scalar_tensor_tensor(
+                    out=planes[g, half][:, t, :],
+                    in0=banks["kv", g, c][:],
+                    scalar=gain_col[:, g - 2, t : t + 1],
+                    in1=banks["bg", g, c][:],
+                    op0=MULT,
+                    op1=ADD,
+                )
+                return
             tile = stage.tile([P, KP], BF16, name="kv_rows", bufs=KV_BUFS)
             kv_rows[g, c] = tile
             nc.vector.scalar_tensor_tensor(
@@ -184,6 +217,17 @@ def tile_qkv_token_compression_d4_kernel(
                 op0=ADD,
                 op1=MULT,
             )
+
+        def interleave(g, pair):
+            half, lo = divmod(pair, 2)
+            tile = stage.tile([P, KP], F32, name="grouped", bufs=8, align_bytes=64)
+            grouped["tk", g, pair] = tile
+            dst = tile[:].bitcast(BF16).rearrange("p (n t) -> p n t", t=4)
+            src = planes[g, half][:, :, 256 * lo : 256 * (lo + 1)].rearrange("p t n -> p n t")
+            if ("il", g, pair) in on_vector:
+                nc.vector.tensor_copy(out=dst, in_=src)
+            else:
+                nc.scalar.copy(out=dst, in_=src)
 
         def turn_kv(g, pair):
             bank = psum.tile([P, 2, 2, P], F32, name="bank")
@@ -204,16 +248,7 @@ def tile_qkv_token_compression_d4_kernel(
         def mul_q(g, j):
             bank = psum.tile([P, D], F32, name="bank")
             banks["q", g, j] = bank
-            for k in range(PASSES):
-                nc.tensor.matmul_mx(
-                    out=bank[:],
-                    lhsT=x_codes[:, g, k, j * P : (j + 1) * P].bitcast(FP8X4),
-                    lhsT_scale=x_plane[:, g, k, j * P : (j + 1) * P],
-                    rhs=wq_codes[:, k, :].bitcast(FP8X4),
-                    rhs_scale=wq_plane[:, k, :],
-                    start=(k == 0),
-                    stop=(k == PASSES - 1),
-                )
+            product(bank, x_operand(g, slice(j * P, (j + 1) * P)), w_operand(0, slice(0, D)))
 
         def empty_q(g, j):
             h, half = divmod(j, 2)
@@ -221,7 +256,10 @@ def tile_qkv_token_compression_d4_kernel(
             if first:
                 q_out[g, h] = stage.tile([P, 2, D], F32, name="q_out", bufs=3)
             nc.vector.tensor_tensor(out=q_out[g, h][:, half, :], in0=banks["q", g, j][:], in1=bias_q[:], op=ADD)
-            if not first:
+            if not first and g in DIRECT:
+                dst = out_q[g * KP : (g + 1) * KP, :].rearrange("(p h e) n -> h p e n", h=2, e=2)
+                nc.sync.dma_start(out=dst[h], in_=q_out[g, h][:])
+            elif not first:
                 dst = out_q[g * KP : (g + 1) * KP, :].rearrange("(a p h e) n -> h e p a n", a=2, h=2, e=2)
                 for e in range(2):
                     nc.sync.dma_start(out=dst[h, e], in_=q_out[g, h][e:P:2])
@@ -257,7 +295,7 @@ def tile_qkv_token_compression_d4_kernel(
         def spread_bias_kv():
             bank = psum.tile([P, 8], F32, name="bank")
             banks["bias_kv"] = bank
-            nc.tensor.matmul(bank[:], lhsT=rows[:, T + D :], rhs=pick[:], start=True, stop=True)
+            nc.tensor.matmul(bank[:], lhsT=rows[:, TG + 3 * D :], rhs=pick[:], start=True, stop=True)
 
         def empty_bias_kv():
             nc.vector.tensor_copy(out=bias_kv[:], in_=banks["bias_kv"][:])
@@ -265,23 +303,35 @@ def tile_qkv_token_compression_d4_kernel(
         def spread_bias_q():
             bank = psum.tile([P, D], BF16, name="bank")
             banks["bias_q"] = bank
-            nc.tensor.matmul(bank[:], lhsT=ones[:, :P], rhs=rows[:, T : T + D], start=True, stop=True)
+            nc.tensor.matmul(bank[:], lhsT=ones[:, :P], rhs=rows[:, TG : TG + D], start=True, stop=True)
 
         def empty_bias_q():
             nc.scalar.copy(out=bias_q[:], in_=banks["bias_q"][:])
+
+        def spread_bias_row(half):
+            bank = psum.tile([P, D], BF16, name="bank")
+            banks["bias_row", half] = bank
+            lo = TG + (1 + half) * D
+            nc.tensor.matmul(bank[:], lhsT=ones[:, :P], rhs=rows[:, lo : lo + D], start=True, stop=True)
+
+        def empty_bias_row(half):
+            nc.scalar.copy(out=bias_row[:, half, :], in_=banks["bias_row", half][:])
+
+        def widen_gain():
+            nc.vector.tensor_copy(out=gain_col[:], in_=gain_raw[:])
 
         def warm(n):
             bank = psum.tile([P, KP], F32, name="bank")
             nc.tensor.matmul(bank[:], lhsT=ones[:, :P], rhs=ones[:], start=True, stop=True)
 
-        nc.scalar.dma_start(out=scale_all[:], in_=w_scale.rearrange("i j -> (i j)").partition_broadcast(P))
+        nc.sync.dma_start(out=scale_all[:], in_=w_scale.rearrange("i j -> (i j)").partition_broadcast(P))
         nc.vector.memset(ones[:], 1.0)
         nc.vector.memset(rows[:].bitcast(I32), 0)
         make_identity(nc, ident[:])
         nc.gpsimd.memset(e_plane[:].rearrange("p g n -> p (g n)").bitcast(U32), 0)
-        nc.scalar.dma_start(out=rows[0:1, 0:T], in_=gain.rearrange("(o t) -> o t", o=1))
-        nc.scalar.dma_start(out=rows[0:1, T : T + D], in_=bias[0:D].rearrange("(o t) -> o t", o=1))
-        nc.scalar.dma_start(out=rows[0:8, T + D :], in_=bias[D:].rearrange("(c p) -> c p", p=P))
+        nc.scalar.dma_start(out=rows[0:1, 0:TG], in_=gain[0:TG].rearrange("(o t) -> o t", o=1))
+        nc.scalar.dma_start(out=rows[0:1, TG : TG + 3 * D], in_=bias.rearrange("(o t) -> o t", o=1))
+        nc.scalar.dma_start(out=rows[0:8, TG + 3 * D :], in_=bias[D:].rearrange("(c p) -> c p", p=P))
         nc.scalar.copy(out=pick[:], in_=ident[:, 0:8])
         for load in LOADS:
             if load[0] == "w":
@@ -296,297 +346,307 @@ def tile_qkv_token_compression_d4_kernel(
             "ex": empty_x, "qx": quant_x, "mk": mul_kv, "ek": empty_kv, "tk": turn_kv, "et": empty_turned_kv,
             "qk": quant_kv, "mq": mul_q, "eq": empty_q, "mz": mul_z, "ez": empty_z, "gain": spread_gain,
             "eg": empty_gain, "bias": spread_bias_kv, "eb": empty_bias_kv, "biasq": spread_bias_q, "ebq": empty_bias_q,
-            "warm": warm,
+            "warm": warm, "bg": bias_gain, "il": interleave, "biask": spread_bias_row, "ebk": empty_bias_row, "gc": widen_gain,
         }
         for step in PLAN:
             steps[step[0]](*step[1:])
 
 
-KV_BUFS = 20
-LOADS = [('w', 4, 2), ('x', 0, 0, 0, 2), ('x', 0, 0, 2, 2), ('x', 0, 1, 0, 2), ('x', 0, 1, 2, 2), ('w', 6, 2), ('x', 1, 0, 0, 4), ('x', 1, 1, 0, 4), ('x', 2, 0, 0, 4), ('x', 2, 1, 0, 4), ('w', 8, 4), ('x', 3, 0, 0, 4), ('x', 3, 1, 0, 4), ('w', 0, 4), ('e',)]
-WIDEN_ON_VECTOR = [3, 7, 8]
-SORTED_GROUPS = [0, 1, 2, 3]
-EMPTY_ON_VECTOR = [('tw', 4), ('tw', 6), ('tx', 0, 0, 1), ('tx', 0, 1, 1), ('tx', 1, 0, 0), ('tx', 1, 1, 0)]
+KV_BUFS = 16
+DIRECT = [2, 3]
+LOADS = [('w', 4, 2), ('x', 0, 0, 0, 2), ('x', 0, 0, 2, 2), ('w', 6, 2), ('x', 0, 1, 0, 2), ('x', 0, 1, 2, 2), ('x', 1, 0, 0, 4), ('x', 1, 1, 0, 4), ('w', 8, 4), ('x', 2, 0, 0, 4), ('x', 3, 0, 0, 4), ('w', 0, 4), ('x', 2, 1, 0, 4), ('x', 3, 1, 0, 4), ('e',)]
+WIDEN_ON_VECTOR = [7, 8, 8]
+SORTED_GROUPS = [0, 1, 2]
+EMPTY_ON_VECTOR = [('il', 3, 3), ('tw', 4), ('tw', 6), ('tx', 0, 0, 1)]
 PLAN = [
     ('wd', 4),
-    ('sx', 0, 0, 0),
-    ('sx', 0, 0, 1),
-    ('sx', 0, 1, 0),
-    ('warm', 0),
-    ('sx', 0, 1, 1),
     ('wd', 5),
+    ('wd', 6),
+    ('warm', 0),
     ('warm', 1),
+    ('sx', 0, 0, 0),
     ('warm', 2),
+    ('sx', 0, 0, 1),
+    ('wd', 7),
     ('gain', 0),
     ('eg', 0),
-    ('wd', 6),
-    ('tw', 4),
-    ('ew', 4),
-    ('wd', 7),
-    ('biasq',),
-    ('ebq',),
+    ('sx', 0, 1, 0),
     ('bias',),
     ('eb',),
+    ('sx', 0, 1, 1),
+    ('biask', 0),
+    ('ebk', 0),
+    ('tw', 4),
+    ('ew', 4),
+    ('tw', 5),
+    ('ew', 5),
     ('qw', 4),
+    ('tw', 6),
+    ('ew', 6),
+    ('qw', 5),
+    ('gain', 1),
+    ('eg', 1),
+    ('qw', 6),
     ('tx', 0, 0, 0),
     ('ex', 0, 0, 0),
     ('tx', 0, 0, 1),
     ('ex', 0, 0, 1),
+    ('qx', 0, 0, 0),
     ('tx', 0, 1, 0),
     ('ex', 0, 1, 0),
-    ('qx', 0, 0, 0),
-    ('tx', 0, 1, 1),
-    ('ex', 0, 1, 1),
     ('sx', 1, 0, 0),
     ('qx', 0, 0, 1),
-    ('tw', 5),
-    ('ew', 5),
+    ('tx', 0, 1, 1),
+    ('ex', 0, 1, 1),
     ('sx', 1, 0, 1),
     ('qx', 0, 1, 0),
-    ('gain', 1),
-    ('eg', 1),
+    ('biasq',),
+    ('ebq',),
     ('sx', 1, 1, 0),
     ('qx', 0, 1, 1),
-    ('gain', 2),
-    ('eg', 2),
+    ('biask', 1),
+    ('ebk', 1),
     ('sx', 1, 1, 1),
-    ('qw', 5),
-    ('tw', 6),
-    ('ew', 6),
+    ('wd', 8),
     ('tw', 7),
     ('ew', 7),
+    ('wd', 9),
     ('mk', 0, 0),
     ('ek', 0, 0),
-    ('qw', 6),
+    ('wd', 10),
     ('qw', 7),
     ('mk', 0, 1),
     ('ek', 0, 1),
-    ('sx', 2, 0, 0),
     ('tx', 1, 0, 0),
     ('ex', 1, 0, 0),
-    ('sx', 2, 0, 1),
     ('tx', 1, 0, 1),
     ('ex', 1, 0, 1),
-    ('sx', 2, 1, 0),
+    ('qx', 1, 0, 0),
     ('tx', 1, 1, 0),
     ('ex', 1, 1, 0),
-    ('sx', 2, 1, 1),
-    ('wd', 8),
-    ('qx', 1, 0, 0),
+    ('qx', 1, 0, 1),
     ('tx', 1, 1, 1),
     ('ex', 1, 1, 1),
-    ('qx', 1, 0, 1),
-    ('gain', 3),
-    ('eg', 3),
+    ('wd', 11),
     ('qx', 1, 1, 0),
     ('mk', 0, 2),
     ('ek', 0, 2),
     ('qx', 1, 1, 1),
     ('mk', 0, 3),
     ('ek', 0, 3),
-    ('tx', 2, 0, 0),
-    ('ex', 2, 0, 0),
-    ('tx', 2, 0, 1),
-    ('ex', 2, 0, 1),
-    ('tx', 2, 1, 0),
-    ('ex', 2, 1, 0),
-    ('wd', 9),
-    ('qx', 2, 0, 0),
-    ('tx', 2, 1, 1),
-    ('ex', 2, 1, 1),
-    ('qx', 2, 0, 1),
+    ('sx', 2, 0, 0),
     ('tw', 8),
     ('ew', 8),
-    ('sx', 3, 0, 0),
-    ('qx', 2, 1, 0),
-    ('mk', 1, 0),
-    ('ek', 1, 0),
-    ('sx', 3, 0, 1),
-    ('qx', 2, 1, 1),
-    ('qw', 8),
-    ('mk', 1, 1),
-    ('ek', 1, 1),
-    ('sx', 3, 1, 0),
-    ('mk', 1, 2),
-    ('ek', 1, 2),
-    ('sx', 3, 1, 1),
-    ('mk', 1, 3),
-    ('ek', 1, 3),
     ('tw', 9),
     ('ew', 9),
-    ('tx', 3, 0, 0),
-    ('ex', 3, 0, 0),
-    ('tx', 3, 0, 1),
-    ('ex', 3, 0, 1),
-    ('qw', 9),
-    ('mk', 2, 0),
-    ('ek', 2, 0),
-    ('qx', 3, 0, 0),
-    ('qx', 3, 0, 1),
-    ('tx', 3, 1, 0),
-    ('ex', 3, 1, 0),
-    ('tx', 3, 1, 1),
-    ('ex', 3, 1, 1),
-    ('tk', 0, 0),
-    ('et', 0, 0),
-    ('qx', 3, 1, 0),
-    ('tk', 0, 1),
-    ('et', 0, 1),
-    ('qx', 3, 1, 1),
-    ('mk', 2, 1),
-    ('ek', 2, 1),
-    ('qk', 0, 0),
-    ('wd', 0),
-    ('qk', 0, 1),
-    ('mk', 2, 2),
-    ('ek', 2, 2),
-    ('wd', 1),
-    ('wd', 10),
-    ('mk', 2, 3),
-    ('ek', 2, 3),
-    ('mk', 3, 0),
-    ('ek', 3, 0),
-    ('mk', 3, 1),
-    ('ek', 3, 1),
-    ('tk', 1, 0),
-    ('et', 1, 0),
-    ('wd', 11),
-    ('tk', 1, 1),
-    ('et', 1, 1),
-    ('wd', 2),
-    ('tw', 0),
-    ('ew', 0),
-    ('wd', 3),
-    ('qk', 1, 0),
-    ('tw', 1),
-    ('ew', 1),
-    ('qk', 1, 1),
+    ('qw', 8),
     ('tw', 10),
     ('ew', 10),
-    ('qw', 0),
-    ('mk', 3, 2),
-    ('ek', 3, 2),
-    ('qw', 1),
+    ('qw', 9),
+    ('mk', 1, 0),
+    ('ek', 1, 0),
     ('qw', 10),
-    ('mk', 3, 3),
-    ('ek', 3, 3),
-    ('mk', 2, 4),
-    ('ek', 2, 4),
+    ('mk', 1, 1),
+    ('ek', 1, 1),
+    ('tx', 2, 0, 0),
+    ('ex', 2, 0, 0),
+    ('wd', 0),
+    ('tx', 3, 0, 0),
+    ('ex', 3, 0, 0),
+    ('wd', 1),
+    ('qx', 2, 0, 0),
     ('tw', 11),
     ('ew', 11),
-    ('tw', 2),
-    ('ew', 2),
-    ('tw', 3),
-    ('ew', 3),
+    ('qx', 3, 0, 0),
+    ('mk', 0, 4),
+    ('ek', 0, 4),
     ('qw', 11),
-    ('tk', 2, 0),
-    ('et', 2, 0),
-    ('qw', 2),
-    ('tk', 2, 1),
-    ('et', 2, 1),
-    ('qw', 3),
-    ('mk', 2, 5),
-    ('ek', 2, 5),
-    ('qk', 2, 0),
-    ('qk', 2, 1),
-    ('mk', 2, 6),
-    ('ek', 2, 6),
-    ('mk', 3, 4),
-    ('ek', 3, 4),
-    ('mk', 3, 5),
-    ('ek', 3, 5),
-    ('tk', 3, 0),
-    ('et', 3, 0),
-    ('tk', 3, 1),
-    ('et', 3, 1),
-    ('mq', 3, 0),
-    ('eq', 3, 0),
-    ('qk', 3, 0),
-    ('qk', 3, 1),
-    ('mq', 3, 1),
-    ('eq', 3, 1),
-    ('mq', 1, 0),
-    ('eq', 1, 0),
-    ('mq', 1, 1),
-    ('eq', 1, 1),
-    ('mq', 1, 2),
-    ('eq', 1, 2),
-    ('mq', 1, 3),
-    ('eq', 1, 3),
-    ('mk', 3, 6),
-    ('ek', 3, 6),
-    ('mk', 3, 7),
-    ('ek', 3, 7),
+    ('mk', 0, 5),
+    ('ek', 0, 5),
+    ('mk', 0, 6),
+    ('ek', 0, 6),
+    ('sx', 2, 0, 1),
+    ('sx', 2, 1, 0),
+    ('mk', 1, 2),
+    ('ek', 1, 2),
+    ('sw', 0),
+    ('mk', 1, 3),
+    ('ek', 1, 3),
+    ('sw', 1),
+    ('tx', 3, 0, 1),
+    ('ex', 3, 0, 1),
+    ('tw', 0),
+    ('ew', 0),
+    ('qx', 3, 0, 1),
+    ('tw', 1),
+    ('ew', 1),
+    ('wd', 2),
+    ('qw', 0),
+    ('tx', 2, 0, 1),
+    ('ex', 2, 0, 1),
+    ('gc',),
+    ('wd', 3),
+    ('qw', 1),
+    ('tx', 2, 1, 0),
+    ('ex', 2, 1, 0),
+    ('qx', 2, 0, 1),
     ('mk', 1, 4),
     ('ek', 1, 4),
+    ('qx', 2, 1, 0),
     ('mk', 1, 5),
     ('ek', 1, 5),
     ('mk', 1, 6),
     ('ek', 1, 6),
     ('mk', 1, 7),
     ('ek', 1, 7),
-    ('mk', 2, 7),
-    ('ek', 2, 7),
-    ('mq', 0, 0),
-    ('eq', 0, 0),
-    ('mq', 0, 1),
-    ('eq', 0, 1),
-    ('mk', 0, 4),
-    ('ek', 0, 4),
-    ('mk', 0, 5),
-    ('ek', 0, 5),
-    ('mk', 0, 6),
-    ('ek', 0, 6),
+    ('sw', 2),
+    ('bg', 2, 0),
     ('mk', 0, 7),
     ('ek', 0, 7),
-    ('mz', 0, 0),
-    ('ez', 0, 0),
-    ('tk', 2, 2),
-    ('et', 2, 2),
-    ('tk', 2, 3),
-    ('et', 2, 3),
-    ('tk', 0, 2),
-    ('et', 0, 2),
-    ('qk', 2, 2),
-    ('tk', 0, 3),
-    ('et', 0, 3),
-    ('qk', 2, 3),
-    ('mq', 2, 0),
-    ('eq', 2, 0),
-    ('qk', 0, 2),
-    ('qk', 0, 3),
-    ('mq', 2, 1),
-    ('eq', 2, 1),
-    ('mq', 2, 2),
-    ('eq', 2, 2),
-    ('mq', 2, 3),
-    ('eq', 2, 3),
-    ('tk', 1, 2),
-    ('et', 1, 2),
-    ('tk', 1, 3),
-    ('et', 1, 3),
-    ('tk', 3, 2),
-    ('et', 3, 2),
-    ('qk', 1, 2),
-    ('tk', 3, 3),
-    ('et', 3, 3),
-    ('qk', 1, 3),
-    ('mq', 3, 2),
-    ('eq', 3, 2),
-    ('qk', 3, 2),
-    ('qk', 3, 3),
-    ('mq', 3, 3),
-    ('eq', 3, 3),
+    ('sw', 3),
+    ('bg', 2, 1),
+    ('sx', 2, 1, 1),
+    ('tx', 3, 1, 0),
+    ('ex', 3, 1, 0),
+    ('tw', 2),
+    ('ew', 2),
+    ('qx', 3, 1, 0),
+    ('tw', 3),
+    ('ew', 3),
+    ('qw', 2),
+    ('tk', 0, 0),
+    ('et', 0, 0),
+    ('qw', 3),
+    ('mk', 2, 0),
+    ('ek', 2, 0),
+    ('qk', 0, 0),
+    ('mk', 2, 1),
+    ('ek', 2, 1),
+    ('tx', 2, 1, 1),
+    ('ex', 2, 1, 1),
+    ('tk', 1, 0),
+    ('et', 1, 0),
+    ('qx', 2, 1, 1),
+    ('tk', 1, 1),
+    ('et', 1, 1),
+    ('qk', 1, 0),
+    ('tx', 3, 1, 1),
+    ('ex', 3, 1, 1),
+    ('bg', 2, 2),
+    ('qk', 1, 1),
+    ('mq', 0, 0),
+    ('eq', 0, 0),
+    ('qx', 3, 1, 1),
+    ('bg', 2, 3),
+    ('mq', 1, 0),
+    ('eq', 1, 0),
+    ('mq', 1, 1),
+    ('eq', 1, 1),
+    ('bg', 3, 0),
+    ('mk', 2, 2),
+    ('ek', 2, 2),
+    ('bg', 3, 1),
+    ('mk', 2, 3),
+    ('ek', 2, 3),
+    ('bg', 3, 2),
+    ('tk', 0, 1),
+    ('et', 0, 1),
+    ('bg', 3, 3),
+    ('mk', 3, 0),
+    ('ek', 3, 0),
+    ('qk', 0, 1),
+    ('mk', 3, 1),
+    ('ek', 3, 1),
+    ('mk', 3, 2),
+    ('ek', 3, 2),
+    ('mk', 3, 3),
+    ('ek', 3, 3),
+    ('il', 2, 0),
+    ('mq', 0, 1),
+    ('eq', 0, 1),
+    ('il', 2, 1),
     ('mq', 0, 2),
     ('eq', 0, 2),
     ('mq', 0, 3),
     ('eq', 0, 3),
+    ('tk', 0, 2),
+    ('et', 0, 2),
+    ('tk', 0, 3),
+    ('et', 0, 3),
+    ('qk', 2, 0),
+    ('qk', 0, 2),
+    ('tk', 1, 2),
+    ('et', 1, 2),
+    ('qk', 2, 1),
+    ('il', 3, 0),
+    ('qk', 0, 3),
+    ('tk', 1, 3),
+    ('et', 1, 3),
+    ('bg', 3, 4),
+    ('il', 3, 1),
+    ('qk', 1, 2),
+    ('mq', 2, 0),
+    ('eq', 2, 0),
+    ('qk', 1, 3),
+    ('bg', 3, 5),
+    ('mq', 2, 1),
+    ('eq', 2, 1),
+    ('bg', 3, 6),
+    ('mq', 2, 2),
+    ('eq', 2, 2),
+    ('bg', 3, 7),
+    ('mk', 3, 4),
+    ('ek', 3, 4),
+    ('qk', 3, 0),
+    ('bg', 2, 4),
+    ('qk', 3, 1),
+    ('mk', 3, 5),
+    ('ek', 3, 5),
+    ('bg', 2, 5),
+    ('mk', 3, 6),
+    ('ek', 3, 6),
+    ('bg', 2, 6),
+    ('mk', 3, 7),
+    ('ek', 3, 7),
+    ('bg', 2, 7),
+    ('mk', 2, 4),
+    ('ek', 2, 4),
+    ('mk', 2, 5),
+    ('ek', 2, 5),
+    ('mk', 2, 6),
+    ('ek', 2, 6),
+    ('mk', 2, 7),
+    ('ek', 2, 7),
+    ('mz', 0, 0),
+    ('ez', 0, 0),
+    ('il', 3, 2),
+    ('il', 3, 3),
+    ('mq', 2, 3),
+    ('eq', 2, 3),
+    ('mq', 1, 2),
+    ('eq', 1, 2),
+    ('mq', 1, 3),
+    ('eq', 1, 3),
+    ('qk', 3, 2),
+    ('il', 2, 2),
+    ('qk', 3, 3),
+    ('il', 2, 3),
     ('mz', 0, 1),
     ('ez', 0, 1),
     ('mz', 0, 2),
     ('ez', 0, 2),
+    ('qk', 2, 2),
+    ('qk', 2, 3),
     ('mz', 0, 3),
     ('ez', 0, 3),
+    ('mq', 3, 0),
+    ('eq', 3, 0),
+    ('mq', 3, 1),
+    ('eq', 3, 1),
+    ('mq', 3, 2),
+    ('eq', 3, 2),
+    ('mq', 3, 3),
+    ('eq', 3, 3),
     ('mz', 1, 0),
     ('ez', 1, 0),
     ('mz', 1, 1),

@@ -20,17 +20,96 @@ COPY = mybir.ActivationFunctionType.Copy
 
 P = 128
 KP = 512
+HALF = KP // 2
 GROUPS = T // KP
 PASSES = C // KP
-W_TILES = 3 * D // P
 BLOCKS = C // P
-TG = 2 * KP
+TILES = D // P
+TURNED = 2
+
+WIDEN_ON_VECTOR = (6, 7, 8)
+SORTED_GROUPS = (0, 2, 3)
+SHARED_BANKS = 5
+
+LOADS = (
+    ("w", 4, 2),
+    ("x", 0, 0, 0, 2),
+    ("w", 6, 2),
+    ("x", 0, 0, 2, 2),
+    ("x", 0, 1, 0, 2),
+    ("x", 0, 1, 2, 2),
+    ("x", 1, 0, 0, 4),
+    ("x", 1, 1, 0, 4),
+    ("w", 8, 4),
+    ("x", 2, 0, 0, 4),
+    ("w", 0, 4),
+    ("x", 2, 1, 0, 4),
+    ("x", 3, 0, 0, 4),
+    ("x", 3, 1, 0, 4),
+)
+
+TENSOR_ORDER = """
+U*3 G0 G1 W1*3 X0*4 X1*4 W1 B K00*3 W2*4 X2*4 T00 K00 W0*4 K11*4 K10*4 K20*3 T11*2 T10*2 X3*4 T00
+K01*4 K20 K30*4 Q2*2 Q3*4 K21*4 T01*2 Q1*4 K31*4 Q2*2 Z0*4 Q0*4 Z1*4
+"""
+
+WIDEN_LEAD = 10
+SORT_LEAD = 12
+BIAS_GAIN_LEAD = 8
+QUANTISE_LAG = 3
+INTERLEAVE_LAG = 5
+INTERLEAVE_STEP = 5
+INTERLEAVED_QUANTISE_LAG = 6
+
+
+def tensor_items():
+    seen = {}
+    items = []
+    for word in TENSOR_ORDER.split():
+        name, count = (word + "*1").split("*")[:2]
+        letter, digits = name[0], [int(d) for d in name[1:]]
+        for n in range(seen.get(name, 0), seen.get(name, 0) + int(count)):
+            if letter == "W":
+                items.append((letter, (TILES * digits[0] + n,)))
+            elif letter == "X":
+                items.append((letter, (digits[0],) + divmod(n, 2)))
+            elif letter in "KTQZ":
+                items.append((letter, tuple(digits) + (n,)))
+            else:
+                items.append((letter, tuple(digits)))
+        seen[name] = seen.get(name, 0) + int(count)
+    return items
+
+
+def program_order():
+    timed = []
+    clock = 0
+    for n, (letter, idx) in enumerate(tensor_items()):
+        if letter == "W":
+            timed.append((clock - WIDEN_LEAD, n, 0, ("widen", letter, idx)))
+        if letter == "X" and idx[0] in SORTED_GROUPS:
+            timed.append((clock - SORT_LEAD, n, 0, ("sort", letter, idx)))
+        if letter == "K" and idx[0] >= TURNED:
+            timed.append((clock - BIAS_GAIN_LEAD, n, 0, ("bias_gain", letter, idx)))
+        timed.append((clock, n, 1, ("tensor", letter, idx)))
+        if letter != "U":
+            timed.append((clock, n, 2, ("empty", letter, idx)))
+        clock += {"K": PASSES, "Q": PASSES, "Z": GROUPS}.get(letter, 1)
+        if letter in "WXT":
+            timed.append((clock + QUANTISE_LAG, n, 3, ("quantise", letter, idx)))
+        if letter == "K" and idx[0] >= TURNED and idx[2] == TILES - 1:
+            for lo in range(2):
+                at = clock + INTERLEAVE_LAG + INTERLEAVE_STEP * lo
+                timed.append((at, n, 3, ("interleave", "T", idx[:2] + (lo,))))
+                timed.append((at + INTERLEAVED_QUANTISE_LAG, n, 4, ("quantise", "T", idx[:2] + (lo,))))
+    return [entry[3] for entry in sorted(timed, key=lambda entry: entry[:3])]
 
 
 def tile_qkv_token_compression_d4_kernel(
     tc, x, w_bytes, w_scale, bias, gain, e_words, e_scales, out_q, out_k, out_v
 ):
     nc = tc.nc
+    turned_tokens = TURNED * KP
     with ExitStack() as ctx:
         keep = ctx.enter_context(tc.tile_pool(name="keep", bufs=1))
         stage = ctx.enter_context(tc.tile_pool(name="stage", bufs=3))
@@ -38,26 +117,27 @@ def tile_qkv_token_compression_d4_kernel(
         ctx.enter_context(tc.manual_schedule())
 
         ident = keep.tile([P, P], F32, name="ident")
-        pick = keep.tile([P, 8], BF16, name="pick")
+        pick = keep.tile([P, 2 * TILES], BF16, name="pick")
         ones = keep.tile([P, KP], BF16, name="ones")
-        rows = keep.tile([P, TG + 3 * D + P], BF16, name="rows")
-        gain_all = keep.tile([P, TG], BF16, name="gain_all")
-        bias_q = keep.tile([P, D], BF16, name="bias_q")
-        bias_kv = keep.tile([P, 8], F32, name="bias_kv")
-        scale_all = keep.tile([P, W_TILES * BLOCKS], F32, name="scale_all")
+        rows = keep.tile([P, turned_tokens + P], BF16, name="rows")
+        gain_rows = keep.tile([P, TURNED, KP], BF16, name="gain_rows")
+        gain_raw = keep.tile([P, GROUPS - TURNED, 4], BF16, name="gain_raw")
+        gain_cols = keep.tile([P, GROUPS - TURNED, 4], F32, name="gain_cols")
+        bias_rows = keep.tile([P, 3, D], BF16, name="bias_rows")
+        bias_cols = keep.tile([P, 2, TILES], F32, name="bias_cols")
+        scale_all = keep.tile([P, 3 * TILES * BLOCKS], F32, name="scale_all")
         e_codes = keep.tile([P, GROUPS, 2 * R], U8, name="e_codes", align_bytes=256)
         e_plane = keep.tile([P, GROUPS, R], U8, name="e_plane", align_bytes=256)
         x_codes = keep.tile([P, GROUPS, PASSES, KP], U32, name="x_codes", align_bytes=256)
         x_plane = keep.tile([P, GROUPS, PASSES, KP], U8, name="x_plane", align_bytes=256)
         w_codes = keep.tile([P, 3, PASSES, D], U32, name="w_codes", align_bytes=256)
         w_plane = keep.tile([P, 3, PASSES, D], U8, name="w_plane", align_bytes=256)
-        bias_row = keep.tile([P, 2, D], BF16, name="bias_row")
-        gain_raw = keep.tile([P, 2, 4], BF16, name="gain_raw")
-        gain_col = keep.tile([P, 2, 4], F32, name="gain_col")
         kv_codes = keep.tile([P, GROUPS, 2, D], U32, name="kv_codes", align_bytes=256)
         kv_plane = keep.tile([P, GROUPS, 2, D], U8, name="kv_plane", align_bytes=256)
 
-        x_raw, w_raw, x_sorted, w_wide, banks, grouped, kv_rows, q_out, planes = {}, {}, {}, {}, {}, {}, {}, {}, {}
+        x_raw, w_raw, x_sorted, w_wide, banks, grouped = {}, {}, {}, {}, {}, {}
+        kv_rows, kv_planes, bias_gains, q_out = {}, {}, {}, {}
+        shared = [item for item in tensor_items() if item[0] in "WXT"][0:SHARED_BANKS:2]
 
         def load_x(g, k, first, count):
             if (g, k) not in x_raw:
@@ -72,30 +152,6 @@ def tile_qkv_token_compression_d4_kernel(
             for i in range(count):
                 w_raw[first + i] = tile[:, i, :]
 
-        def load_e():
-            nc.sync.dma_start(out=gain_raw[:], in_=gain[TG:].rearrange("(g p t) -> p g t", p=P, t=4))
-            nc.sync.dma_start(out=e_codes[:].bitcast(I32), in_=e_words.rearrange("g p n -> p g n").bitcast(I32))
-            for q in range(4):
-                nc.sync.dma_start(
-                    out=e_plane[32 * q : 32 * q + 4].bitcast(I32),
-                    in_=e_scales[:, 4 * q : 4 * q + 4, :].rearrange("g r n -> r g n").bitcast(I32),
-                )
-
-        on_vector = set(EMPTY_ON_VECTOR)
-
-        def empty(key, order):
-            tile = stage.tile([P, KP], F32, name="grouped", bufs=8, align_bytes=64)
-            grouped[key] = tile
-            src = banks[key][:].rearrange(order)
-            dst = tile[:].rearrange("p (a b c) -> p a b c", a=src.shape[1], b=src.shape[2])
-            if key in on_vector:
-                nc.vector.tensor_copy(out=dst, in_=src)
-            else:
-                nc.scalar.copy(out=dst, in_=src)
-
-        def quantise(codes, plane, words):
-            nc.vector.quantize_mx(out=codes.bitcast(FP8X4), scales=plane, in_=words.bitcast(BF16))
-
         def widen(i):
             wide = stage.tile([P, C], BF16, name="w_wide", bufs=6)
             w_wide[i] = wide
@@ -103,64 +159,43 @@ def tile_qkv_token_compression_d4_kernel(
                 cols = slice(j * P, (j + 1) * P)
                 scale = scale_all[:, i * BLOCKS + j : i * BLOCKS + j + 1]
                 src = w_raw[i][:, cols].bitcast(FP8)
-                if j < WIDEN_ON_VECTOR[i // 4]:
+                if j < WIDEN_ON_VECTOR[i // TILES]:
                     nc.vector.tensor_scalar(out=wide[:, cols], in0=src, scalar1=scale, scalar2=None, op0=MULT)
                 else:
                     nc.scalar.activation(out=wide[:, cols], in_=src, func=COPY, scale=scale)
 
-        def sort_w(i):
-            tile = stage.tile([P, 2, 2, P], F32, name="x_sorted", bufs=6)
-            x_sorted["w", i] = tile
-            nc.scalar.copy(out=tile[:], in_=w_wide[i][:].bitcast(F32).rearrange("p (k q u) -> p k u q", k=2, u=2))
-
-        def turn_w(i):
-            bank = psum.tile([P, PASSES, 2, P], F32, name="bank")
-            banks["tw", i] = bank
-            words = w_wide[i][:].bitcast(F32)
-            for k in range(PASSES):
-                for u in range(2):
-                    if ("w", i) in x_sorted:
-                        src = x_sorted["w", i][:, k, u, :]
-                    else:
-                        src = words[:, 256 * k + u : 256 * (k + 1) : 2]
-                    nc.tensor.transpose(bank[:, k, u, :], src, ident[:])
-
-        def empty_w(i):
-            empty(("tw", i), "p k u n -> p k n u")
-
-        def quant_w(i):
-            part, lo = divmod(i, 4)
-            cols = slice(lo * P, (lo + 1) * P)
-            for k in range(PASSES):
-                words = grouped["tw", i][:, 256 * k : 256 * (k + 1)]
-                quantise(w_codes[:, part, k, cols], w_plane[:, part, k, cols], words)
-
         def sort_x(g, k, h):
             tile = stage.tile([P, 2, 2, P], F32, name="x_sorted", bufs=6)
             x_sorted[g, k, h] = tile
-            words = x_raw[g, k][:, 2 * h : 2 * h + 2, :].rearrange("p e c -> p (e c)").bitcast(F32)
-            nc.scalar.copy(out=tile[:], in_=words.rearrange("p (e q u) -> p e u q", e=2, u=2))
+            pairs = x_raw[g, k][:, 2 * h : 2 * h + 2, :].rearrange("p e c -> p (e c)").bitcast(F32)
+            nc.scalar.copy(out=tile[:], in_=pairs.rearrange("p (e q u) -> p e u q", e=2, u=2))
 
-        def turn_x(g, k, h):
+        def bias_gain(g, h, t):
+            tile = stage.tile([P, D], F32, name="bias_gain", bufs=6)
+            bias_gains[g, h, t] = tile
+            scale = gain_cols[:, g - TURNED, t : t + 1]
+            nc.scalar.activation(out=tile[:], in_=bias_rows[:, 1 + h, :], func=COPY, scale=scale)
+
+        def turn(letter, idx):
             bank = psum.tile([P, 2, 2, P], F32, name="bank")
-            banks["tx", g, k, h] = bank
-            for e in range(2):
+            for a in range(2):
                 for u in range(2):
-                    if g in SORTED_GROUPS:
-                        src = x_sorted[g, k, h][:, e, u, :]
+                    if letter == "W":
+                        src = w_wide[idx[0]][:].bitcast(F32)[:, HALF * a + u : HALF * (a + 1) : 2]
+                    elif letter == "X" and idx in x_sorted:
+                        src = x_sorted[idx][:, a, u, :]
+                    elif letter == "X":
+                        g, k, h = idx
+                        src = x_raw[g, k][:, 2 * h + a, :].bitcast(F32)[:, u:HALF:2]
                     else:
-                        src = x_raw[g, k][:, 2 * h + e, :].bitcast(F32)[:, u:256:2]
-                    nc.tensor.transpose(bank[:, e, u, :], src, ident[:])
+                        g, h, lo = idx
+                        src = kv_rows[g, h, 2 * lo + a][:].bitcast(F32)[:, u * P : (u + 1) * P]
+                    nc.tensor.transpose(bank[:, a, u, :], src, ident[:])
+            return bank
 
-        def empty_x(g, k, h):
-            empty(("tx", g, k, h), "q e u p -> q e p u" if g in DIRECT else "q e u p -> q p e u")
-
-        def quant_x(g, k, h):
-            cols = slice(256 * h, 256 * (h + 1))
-            quantise(x_codes[:, g, k, cols], x_plane[:, g, k, cols], grouped["tx", g, k, h][:])
-
-        def product(bank, lhs, rhs):
-            for k, ((a, a_plane), (b, b_plane)) in enumerate(zip(lhs, rhs)):
+        def product(stationary, moving):
+            bank = psum.tile([P, KP], F32, name="bank")
+            for k, ((a, a_plane), (b, b_plane)) in enumerate(zip(stationary, moving)):
                 nc.tensor.matmul_mx(
                     out=bank[:],
                     lhsT=a,
@@ -168,8 +203,9 @@ def tile_qkv_token_compression_d4_kernel(
                     rhs=b,
                     rhs_scale=b_plane,
                     start=(k == 0),
-                    stop=(k == len(lhs) - 1),
+                    stop=(k == len(moving) - 1),
                 )
+            return bank
 
         def x_operand(g, cols):
             return [(x_codes[:, g, k, cols].bitcast(FP8X4), x_plane[:, g, k, cols]) for k in range(PASSES)]
@@ -177,482 +213,155 @@ def tile_qkv_token_compression_d4_kernel(
         def w_operand(part, cols):
             return [(w_codes[:, part, k, cols].bitcast(FP8X4), w_plane[:, part, k, cols]) for k in range(PASSES)]
 
-        def mul_kv(g, c):
-            bank = psum.tile([P, KP], F32, name="bank")
-            banks["kv", g, c] = bank
-            half, i = divmod(c, 4)
-            cols = slice(i * P, (i + 1) * P)
-            if g in DIRECT:
-                product(bank, x_operand(g, cols), w_operand(1 + half, slice(0, D)))
+        def tensor(letter, idx):
+            everything = slice(0, KP)
+            tile_cols = slice(idx[-1] * P, (idx[-1] + 1) * P) if letter in "KQZ" else None
+            if letter in "WXT":
+                bank = turn(letter, idx)
+            elif letter == "Q":
+                bank = product(x_operand(idx[0], tile_cols), w_operand(0, everything))
+            elif letter == "K" and idx[0] >= TURNED:
+                bank = product(x_operand(idx[0], tile_cols), w_operand(1 + idx[1], everything))
+            elif letter == "K":
+                bank = product(w_operand(1 + idx[1], tile_cols), x_operand(idx[0], everything))
+            elif letter == "Z":
+                h, r = idx
+                words = slice(2 * r * P, 2 * (r + 1) * P)
+                e_operand = [(e_codes[:, g, words].bitcast(FP4X4), e_plane[:, g, tile_cols]) for g in range(GROUPS)]
+                kv_operand = [(kv_codes[:, g, h, :].bitcast(FP8X4), kv_plane[:, g, h, :]) for g in range(GROUPS)]
+                bank = product(e_operand, kv_operand)
+            elif letter == "G":
+                bank = psum.tile([P, KP], BF16, name="bank")
+                src = rows[:, idx[0] * KP : (idx[0] + 1) * KP].rearrange("r (p u e) -> r u p e", u=2, e=2)
+                nc.tensor.matmul(bank[:], lhsT=ones[:, :P], rhs=src, start=True, stop=True)
+            elif letter == "B":
+                bank = psum.tile([P, 2 * TILES], F32, name="bank")
+                nc.tensor.matmul(bank[:], lhsT=rows[:, turned_tokens:], rhs=pick[:], start=True, stop=True)
             else:
-                product(bank, w_operand(1 + half, cols), x_operand(g, slice(0, KP)))
+                bank = psum.tile([P, KP], F32, name="bank")
+                nc.tensor.matmul(bank[:], lhsT=ones[:, :P], rhs=ones[:], start=True, stop=True)
+            banks[letter, idx] = bank
 
-        def bias_gain(g, c):
-            half, t = divmod(c, 4)
-            tile = stage.tile([P, D], F32, name="bias_gain", bufs=6)
-            banks["bg", g, c] = tile
-            nc.scalar.activation(out=tile[:], in_=bias_row[:, half, :], func=COPY, scale=gain_col[:, g - 2, t : t + 1])
-
-        def empty_kv(g, c):
-            if g in DIRECT:
-                half, t = divmod(c, 4)
-                if (g, half) not in planes:
-                    planes[g, half] = stage.tile([P, 4, D], BF16, name="planes", bufs=3)
-                nc.vector.scalar_tensor_tensor(
-                    out=planes[g, half][:, t, :],
-                    in0=banks["kv", g, c][:],
-                    scalar=gain_col[:, g - 2, t : t + 1],
-                    in1=banks["bg", g, c][:],
-                    op0=MULT,
-                    op1=ADD,
-                )
-                return
-            tile = stage.tile([P, KP], BF16, name="kv_rows", bufs=KV_BUFS)
-            kv_rows[g, c] = tile
-            nc.vector.scalar_tensor_tensor(
-                out=tile[:],
-                in0=banks["kv", g, c][:],
-                scalar=bias_kv[:, c : c + 1],
-                in1=gain_all[:, g * KP : (g + 1) * KP],
-                op0=ADD,
-                op1=MULT,
-            )
-
-        def interleave(g, pair):
-            half, lo = divmod(pair, 2)
+        def empty_turned(letter, idx):
             tile = stage.tile([P, KP], F32, name="grouped", bufs=8, align_bytes=64)
-            grouped["tk", g, pair] = tile
-            dst = tile[:].bitcast(BF16).rearrange("p (n t) -> p n t", t=4)
-            src = planes[g, half][:, :, 256 * lo : 256 * (lo + 1)].rearrange("p t n -> p n t")
-            if ("il", g, pair) in on_vector:
+            grouped[letter, idx] = tile
+            if letter == "X" and idx[0] < TURNED:
+                src = banks[letter, idx][:].rearrange("p a u n -> p n a u")
+            else:
+                src = banks[letter, idx][:].rearrange("p a u n -> p a n u")
+            dst = tile[:].rearrange("p (a b c) -> p a b c", a=src.shape[1], b=src.shape[2])
+            if (letter, idx) in shared:
                 nc.vector.tensor_copy(out=dst, in_=src)
             else:
                 nc.scalar.copy(out=dst, in_=src)
 
-        def turn_kv(g, pair):
-            bank = psum.tile([P, 2, 2, P], F32, name="bank")
-            banks["tk", g, pair] = bank
-            for i in range(2):
-                words = kv_rows[g, 2 * pair + i][:].bitcast(F32)
-                for h in range(2):
-                    nc.tensor.transpose(bank[:, i, h, :], words[:, h * P : (h + 1) * P], ident[:])
-
-        def empty_turned_kv(g, pair):
-            empty(("tk", g, pair), "p i h n -> p i n h")
-
-        def quant_kv(g, pair):
-            half, lo = divmod(pair, 2)
-            cols = slice(256 * lo, 256 * (lo + 1))
-            quantise(kv_codes[:, g, half, cols], kv_plane[:, g, half, cols], grouped["tk", g, pair][:])
-
-        def mul_q(g, j):
-            bank = psum.tile([P, D], F32, name="bank")
-            banks["q", g, j] = bank
-            product(bank, x_operand(g, slice(j * P, (j + 1) * P)), w_operand(0, slice(0, D)))
-
-        def empty_q(g, j):
-            h, half = divmod(j, 2)
-            first = (g, h) not in q_out
-            if first:
-                q_out[g, h] = stage.tile([P, 2, D], F32, name="q_out", bufs=3)
-            nc.vector.tensor_tensor(out=q_out[g, h][:, half, :], in0=banks["q", g, j][:], in1=bias_q[:], op=ADD)
-            if not first and g in DIRECT:
-                dst = out_q[g * KP : (g + 1) * KP, :].rearrange("(p h e) n -> h p e n", h=2, e=2)
-                nc.sync.dma_start(out=dst[h], in_=q_out[g, h][:])
-            elif not first:
-                dst = out_q[g * KP : (g + 1) * KP, :].rearrange("(a p h e) n -> h e p a n", a=2, h=2, e=2)
-                for e in range(2):
-                    nc.sync.dma_start(out=dst[h, e], in_=q_out[g, h][e:P:2])
-
-        def mul_z(half, r):
-            bank = psum.tile([P, D], F32, name="bank")
-            banks["z", half, r] = bank
-            for g in range(GROUPS):
-                nc.tensor.matmul_mx(
-                    out=bank[:],
-                    lhsT=e_codes[:, g, 2 * r * P : 2 * (r + 1) * P].bitcast(FP4X4),
-                    lhsT_scale=e_plane[:, g, r * P : (r + 1) * P],
-                    rhs=kv_codes[:, g, half, :].bitcast(FP8X4),
-                    rhs_scale=kv_plane[:, g, half, :],
-                    start=(g == 0),
-                    stop=(g == GROUPS - 1),
+        def empty_kv(g, h, i):
+            bank = banks["K", (g, h, i)]
+            if g < TURNED:
+                tile = stage.tile([P, KP], BF16, name="kv_rows", bufs=TURNED * 2 * TILES)
+                kv_rows[g, h, i] = tile
+                nc.vector.scalar_tensor_tensor(
+                    out=tile[:], in0=bank[:], scalar=bias_cols[:, h, i : i + 1], in1=gain_rows[:, g, :], op0=ADD, op1=MULT
+                )
+            else:
+                if i == 0:
+                    kv_planes[g, h] = stage.tile([P, 4, D], BF16, name="kv_planes")
+                nc.vector.scalar_tensor_tensor(
+                    out=kv_planes[g, h][:, i, :],
+                    in0=bank[:],
+                    scalar=gain_cols[:, g - TURNED, i : i + 1],
+                    in1=bias_gains[g, h, i][:],
+                    op0=MULT,
+                    op1=ADD,
                 )
 
-        def empty_z(half, r):
-            tile = stage.tile([P, D], F32, name="z_out", bufs=4)
-            nc.scalar.copy(out=tile[:], in_=banks["z", half, r][:])
-            nc.sync.dma_start(out=(out_k, out_v)[half][r * P : (r + 1) * P, :], in_=tile[:])
+        def empty_q(g, j):
+            u, a = divmod(j, 2)
+            if a == 0:
+                q_out[g, u] = stage.tile([P, 2, D], F32, name="q_out")
+            nc.vector.tensor_tensor(out=q_out[g, u][:, a, :], in0=banks["Q", (g, j)][:], in1=bias_rows[:, 0, :], op=ADD)
+            if a == 0:
+                return
+            group_rows = out_q[g * KP : (g + 1) * KP, :]
+            if g < TURNED:
+                dst = group_rows.rearrange("(a p u e) n -> u e p a n", a=2, u=2, e=2)
+                for e in range(2):
+                    nc.sync.dma_start(out=dst[u, e], in_=q_out[g, u][e:P:2])
+            else:
+                dst = group_rows.rearrange("(p u a) n -> u p a n", u=2, a=2)
+                nc.sync.dma_start(out=dst[u], in_=q_out[g, u][:])
 
-        def spread_gain(g):
-            bank = psum.tile([P, KP], BF16, name="bank")
-            banks["gain", g] = bank
-            src = rows[:, g * KP : (g + 1) * KP].rearrange("r (p h e) -> r h p e", h=2, e=2)
-            nc.tensor.matmul(bank[:], lhsT=ones[:, :P], rhs=src, start=True, stop=True)
+        def empty(letter, idx):
+            bank = banks[letter, idx]
+            if letter in "WXT":
+                empty_turned(letter, idx)
+            elif letter == "K":
+                empty_kv(*idx)
+            elif letter == "Q":
+                empty_q(*idx)
+            elif letter == "Z":
+                h, r = idx
+                tile = stage.tile([P, D], F32, name="z_out", bufs=4)
+                nc.scalar.copy(out=tile[:], in_=bank[:])
+                nc.sync.dma_start(out=(out_k, out_v)[h][r * P : (r + 1) * P, :], in_=tile[:])
+            elif letter == "G":
+                nc.scalar.copy(out=gain_rows[:, idx[0], :], in_=bank[:])
+            else:
+                nc.vector.tensor_copy(out=bias_cols[:].rearrange("p h i -> p (h i)"), in_=bank[:])
+                nc.vector.tensor_copy(out=gain_cols[:], in_=gain_raw[:])
 
-        def empty_gain(g):
-            nc.scalar.copy(out=gain_all[:, g * KP : (g + 1) * KP], in_=banks["gain", g][:])
+        def interleave(g, h, lo):
+            tile = stage.tile([P, KP], F32, name="grouped", bufs=8, align_bytes=64)
+            grouped["T", (g, h, lo)] = tile
+            dst = tile[:].bitcast(BF16).rearrange("p (n t) -> p n t", t=4)
+            src = kv_planes[g, h][:, :, HALF * lo : HALF * (lo + 1)].rearrange("p t n -> p n t")
+            if (g, h) == (GROUPS - 1, 1):
+                nc.vector.tensor_copy(out=dst, in_=src)
+            else:
+                nc.scalar.copy(out=dst, in_=src)
 
-        def spread_bias_kv():
-            bank = psum.tile([P, 8], F32, name="bank")
-            banks["bias_kv"] = bank
-            nc.tensor.matmul(bank[:], lhsT=rows[:, TG + 3 * D :], rhs=pick[:], start=True, stop=True)
-
-        def empty_bias_kv():
-            nc.vector.tensor_copy(out=bias_kv[:], in_=banks["bias_kv"][:])
-
-        def spread_bias_q():
-            bank = psum.tile([P, D], BF16, name="bank")
-            banks["bias_q"] = bank
-            nc.tensor.matmul(bank[:], lhsT=ones[:, :P], rhs=rows[:, TG : TG + D], start=True, stop=True)
-
-        def empty_bias_q():
-            nc.scalar.copy(out=bias_q[:], in_=banks["bias_q"][:])
-
-        def spread_bias_row(half):
-            bank = psum.tile([P, D], BF16, name="bank")
-            banks["bias_row", half] = bank
-            lo = TG + (1 + half) * D
-            nc.tensor.matmul(bank[:], lhsT=ones[:, :P], rhs=rows[:, lo : lo + D], start=True, stop=True)
-
-        def empty_bias_row(half):
-            nc.scalar.copy(out=bias_row[:, half, :], in_=banks["bias_row", half][:])
-
-        def widen_gain():
-            nc.vector.tensor_copy(out=gain_col[:], in_=gain_raw[:])
-
-        def warm(n):
-            bank = psum.tile([P, KP], F32, name="bank")
-            nc.tensor.matmul(bank[:], lhsT=ones[:, :P], rhs=ones[:], start=True, stop=True)
+        def quantise(letter, idx):
+            pairs = grouped[letter, idx]
+            if letter == "W":
+                part, i = divmod(idx[0], TILES)
+                cols = slice(i * P, (i + 1) * P)
+                jobs = [
+                    (w_codes[:, part, k, cols], w_plane[:, part, k, cols], pairs[:, HALF * k : HALF * (k + 1)])
+                    for k in range(PASSES)
+                ]
+            else:
+                codes, plane = (x_codes, x_plane) if letter == "X" else (kv_codes, kv_plane)
+                cols = slice(HALF * idx[2], HALF * (idx[2] + 1))
+                jobs = [(codes[:, idx[0], idx[1], cols], plane[:, idx[0], idx[1], cols], pairs[:])]
+            for codes_out, plane_out, src in jobs:
+                nc.vector.quantize_mx(out=codes_out.bitcast(FP8X4), scales=plane_out, in_=src.bitcast(BF16))
 
         nc.sync.dma_start(out=scale_all[:], in_=w_scale.rearrange("i j -> (i j)").partition_broadcast(P))
         nc.vector.memset(ones[:], 1.0)
         nc.vector.memset(rows[:].bitcast(I32), 0)
         make_identity(nc, ident[:])
         nc.gpsimd.memset(e_plane[:].rearrange("p g n -> p (g n)").bitcast(U32), 0)
-        nc.scalar.dma_start(out=rows[0:1, 0:TG], in_=gain[0:TG].rearrange("(o t) -> o t", o=1))
-        nc.scalar.dma_start(out=rows[0:1, TG : TG + 3 * D], in_=bias.rearrange("(o t) -> o t", o=1))
-        nc.scalar.dma_start(out=rows[0:8, TG + 3 * D :], in_=bias[D:].rearrange("(c p) -> c p", p=P))
-        nc.scalar.copy(out=pick[:], in_=ident[:, 0:8])
+        nc.scalar.dma_start(out=rows[0:1, 0:turned_tokens], in_=gain[0:turned_tokens].rearrange("(o t) -> o t", o=1))
+        nc.scalar.dma_start(out=rows[0 : 2 * TILES, turned_tokens:], in_=bias[D:].rearrange("(i p) -> i p", p=P))
+        nc.scalar.dma_start(out=gain_raw[:], in_=gain[turned_tokens:].rearrange("(g p t) -> p g t", p=P, t=4))
+        nc.scalar.copy(out=pick[:], in_=ident[:, 0 : 2 * TILES])
         for load in LOADS:
             if load[0] == "w":
-                load_w(load[1], load[2])
-            elif load[0] == "x":
-                load_x(*load[1:])
+                load_w(*load[1:])
             else:
-                load_e()
+                load_x(*load[1:])
+        nc.sync.dma_start(out=bias_rows[:].rearrange("p a n -> p (a n)"), in_=bias.partition_broadcast(P))
+        nc.sync.dma_start(out=e_codes[:].bitcast(I32), in_=e_words.rearrange("g p n -> p g n").bitcast(I32))
+        for q in range(4):
+            nc.sync.dma_start(
+                out=e_plane[32 * q : 32 * q + 4].bitcast(I32),
+                in_=e_scales[:, 4 * q : 4 * q + 4, :].rearrange("g r n -> r g n").bitcast(I32),
+            )
 
-        steps = {
-            "wd": widen, "tw": turn_w, "ew": empty_w, "qw": quant_w, "sx": sort_x, "sw": sort_w, "tx": turn_x,
-            "ex": empty_x, "qx": quant_x, "mk": mul_kv, "ek": empty_kv, "tk": turn_kv, "et": empty_turned_kv,
-            "qk": quant_kv, "mq": mul_q, "eq": empty_q, "mz": mul_z, "ez": empty_z, "gain": spread_gain,
-            "eg": empty_gain, "bias": spread_bias_kv, "eb": empty_bias_kv, "biasq": spread_bias_q, "ebq": empty_bias_q,
-            "warm": warm, "bg": bias_gain, "il": interleave, "biask": spread_bias_row, "ebk": empty_bias_row, "gc": widen_gain,
-        }
-        for step in PLAN:
-            steps[step[0]](*step[1:])
-
-
-KV_BUFS = 16
-DIRECT = [2, 3]
-LOADS = [('w', 4, 2), ('x', 0, 0, 0, 2), ('x', 0, 0, 2, 2), ('w', 6, 2), ('x', 0, 1, 0, 2), ('x', 0, 1, 2, 2), ('x', 1, 0, 0, 4), ('x', 1, 1, 0, 4), ('w', 8, 4), ('x', 2, 0, 0, 4), ('x', 3, 0, 0, 4), ('w', 0, 4), ('x', 2, 1, 0, 4), ('x', 3, 1, 0, 4), ('e',)]
-WIDEN_ON_VECTOR = [7, 8, 8]
-SORTED_GROUPS = [0, 1, 2]
-EMPTY_ON_VECTOR = [('il', 3, 3), ('tw', 4), ('tw', 6), ('tx', 0, 0, 1)]
-PLAN = [
-    ('wd', 4),
-    ('wd', 5),
-    ('wd', 6),
-    ('warm', 0),
-    ('warm', 1),
-    ('sx', 0, 0, 0),
-    ('warm', 2),
-    ('sx', 0, 0, 1),
-    ('wd', 7),
-    ('gain', 0),
-    ('eg', 0),
-    ('sx', 0, 1, 0),
-    ('bias',),
-    ('eb',),
-    ('sx', 0, 1, 1),
-    ('biask', 0),
-    ('ebk', 0),
-    ('tw', 4),
-    ('ew', 4),
-    ('tw', 5),
-    ('ew', 5),
-    ('qw', 4),
-    ('tw', 6),
-    ('ew', 6),
-    ('qw', 5),
-    ('gain', 1),
-    ('eg', 1),
-    ('qw', 6),
-    ('tx', 0, 0, 0),
-    ('ex', 0, 0, 0),
-    ('tx', 0, 0, 1),
-    ('ex', 0, 0, 1),
-    ('qx', 0, 0, 0),
-    ('tx', 0, 1, 0),
-    ('ex', 0, 1, 0),
-    ('sx', 1, 0, 0),
-    ('qx', 0, 0, 1),
-    ('tx', 0, 1, 1),
-    ('ex', 0, 1, 1),
-    ('sx', 1, 0, 1),
-    ('qx', 0, 1, 0),
-    ('biasq',),
-    ('ebq',),
-    ('sx', 1, 1, 0),
-    ('qx', 0, 1, 1),
-    ('biask', 1),
-    ('ebk', 1),
-    ('sx', 1, 1, 1),
-    ('wd', 8),
-    ('tw', 7),
-    ('ew', 7),
-    ('wd', 9),
-    ('mk', 0, 0),
-    ('ek', 0, 0),
-    ('wd', 10),
-    ('qw', 7),
-    ('mk', 0, 1),
-    ('ek', 0, 1),
-    ('tx', 1, 0, 0),
-    ('ex', 1, 0, 0),
-    ('tx', 1, 0, 1),
-    ('ex', 1, 0, 1),
-    ('qx', 1, 0, 0),
-    ('tx', 1, 1, 0),
-    ('ex', 1, 1, 0),
-    ('qx', 1, 0, 1),
-    ('tx', 1, 1, 1),
-    ('ex', 1, 1, 1),
-    ('wd', 11),
-    ('qx', 1, 1, 0),
-    ('mk', 0, 2),
-    ('ek', 0, 2),
-    ('qx', 1, 1, 1),
-    ('mk', 0, 3),
-    ('ek', 0, 3),
-    ('sx', 2, 0, 0),
-    ('tw', 8),
-    ('ew', 8),
-    ('tw', 9),
-    ('ew', 9),
-    ('qw', 8),
-    ('tw', 10),
-    ('ew', 10),
-    ('qw', 9),
-    ('mk', 1, 0),
-    ('ek', 1, 0),
-    ('qw', 10),
-    ('mk', 1, 1),
-    ('ek', 1, 1),
-    ('tx', 2, 0, 0),
-    ('ex', 2, 0, 0),
-    ('wd', 0),
-    ('tx', 3, 0, 0),
-    ('ex', 3, 0, 0),
-    ('wd', 1),
-    ('qx', 2, 0, 0),
-    ('tw', 11),
-    ('ew', 11),
-    ('qx', 3, 0, 0),
-    ('mk', 0, 4),
-    ('ek', 0, 4),
-    ('qw', 11),
-    ('mk', 0, 5),
-    ('ek', 0, 5),
-    ('mk', 0, 6),
-    ('ek', 0, 6),
-    ('sx', 2, 0, 1),
-    ('sx', 2, 1, 0),
-    ('mk', 1, 2),
-    ('ek', 1, 2),
-    ('sw', 0),
-    ('mk', 1, 3),
-    ('ek', 1, 3),
-    ('sw', 1),
-    ('tx', 3, 0, 1),
-    ('ex', 3, 0, 1),
-    ('tw', 0),
-    ('ew', 0),
-    ('qx', 3, 0, 1),
-    ('tw', 1),
-    ('ew', 1),
-    ('wd', 2),
-    ('qw', 0),
-    ('tx', 2, 0, 1),
-    ('ex', 2, 0, 1),
-    ('gc',),
-    ('wd', 3),
-    ('qw', 1),
-    ('tx', 2, 1, 0),
-    ('ex', 2, 1, 0),
-    ('qx', 2, 0, 1),
-    ('mk', 1, 4),
-    ('ek', 1, 4),
-    ('qx', 2, 1, 0),
-    ('mk', 1, 5),
-    ('ek', 1, 5),
-    ('mk', 1, 6),
-    ('ek', 1, 6),
-    ('mk', 1, 7),
-    ('ek', 1, 7),
-    ('sw', 2),
-    ('bg', 2, 0),
-    ('mk', 0, 7),
-    ('ek', 0, 7),
-    ('sw', 3),
-    ('bg', 2, 1),
-    ('sx', 2, 1, 1),
-    ('tx', 3, 1, 0),
-    ('ex', 3, 1, 0),
-    ('tw', 2),
-    ('ew', 2),
-    ('qx', 3, 1, 0),
-    ('tw', 3),
-    ('ew', 3),
-    ('qw', 2),
-    ('tk', 0, 0),
-    ('et', 0, 0),
-    ('qw', 3),
-    ('mk', 2, 0),
-    ('ek', 2, 0),
-    ('qk', 0, 0),
-    ('mk', 2, 1),
-    ('ek', 2, 1),
-    ('tx', 2, 1, 1),
-    ('ex', 2, 1, 1),
-    ('tk', 1, 0),
-    ('et', 1, 0),
-    ('qx', 2, 1, 1),
-    ('tk', 1, 1),
-    ('et', 1, 1),
-    ('qk', 1, 0),
-    ('tx', 3, 1, 1),
-    ('ex', 3, 1, 1),
-    ('bg', 2, 2),
-    ('qk', 1, 1),
-    ('mq', 0, 0),
-    ('eq', 0, 0),
-    ('qx', 3, 1, 1),
-    ('bg', 2, 3),
-    ('mq', 1, 0),
-    ('eq', 1, 0),
-    ('mq', 1, 1),
-    ('eq', 1, 1),
-    ('bg', 3, 0),
-    ('mk', 2, 2),
-    ('ek', 2, 2),
-    ('bg', 3, 1),
-    ('mk', 2, 3),
-    ('ek', 2, 3),
-    ('bg', 3, 2),
-    ('tk', 0, 1),
-    ('et', 0, 1),
-    ('bg', 3, 3),
-    ('mk', 3, 0),
-    ('ek', 3, 0),
-    ('qk', 0, 1),
-    ('mk', 3, 1),
-    ('ek', 3, 1),
-    ('mk', 3, 2),
-    ('ek', 3, 2),
-    ('mk', 3, 3),
-    ('ek', 3, 3),
-    ('il', 2, 0),
-    ('mq', 0, 1),
-    ('eq', 0, 1),
-    ('il', 2, 1),
-    ('mq', 0, 2),
-    ('eq', 0, 2),
-    ('mq', 0, 3),
-    ('eq', 0, 3),
-    ('tk', 0, 2),
-    ('et', 0, 2),
-    ('tk', 0, 3),
-    ('et', 0, 3),
-    ('qk', 2, 0),
-    ('qk', 0, 2),
-    ('tk', 1, 2),
-    ('et', 1, 2),
-    ('qk', 2, 1),
-    ('il', 3, 0),
-    ('qk', 0, 3),
-    ('tk', 1, 3),
-    ('et', 1, 3),
-    ('bg', 3, 4),
-    ('il', 3, 1),
-    ('qk', 1, 2),
-    ('mq', 2, 0),
-    ('eq', 2, 0),
-    ('qk', 1, 3),
-    ('bg', 3, 5),
-    ('mq', 2, 1),
-    ('eq', 2, 1),
-    ('bg', 3, 6),
-    ('mq', 2, 2),
-    ('eq', 2, 2),
-    ('bg', 3, 7),
-    ('mk', 3, 4),
-    ('ek', 3, 4),
-    ('qk', 3, 0),
-    ('bg', 2, 4),
-    ('qk', 3, 1),
-    ('mk', 3, 5),
-    ('ek', 3, 5),
-    ('bg', 2, 5),
-    ('mk', 3, 6),
-    ('ek', 3, 6),
-    ('bg', 2, 6),
-    ('mk', 3, 7),
-    ('ek', 3, 7),
-    ('bg', 2, 7),
-    ('mk', 2, 4),
-    ('ek', 2, 4),
-    ('mk', 2, 5),
-    ('ek', 2, 5),
-    ('mk', 2, 6),
-    ('ek', 2, 6),
-    ('mk', 2, 7),
-    ('ek', 2, 7),
-    ('mz', 0, 0),
-    ('ez', 0, 0),
-    ('il', 3, 2),
-    ('il', 3, 3),
-    ('mq', 2, 3),
-    ('eq', 2, 3),
-    ('mq', 1, 2),
-    ('eq', 1, 2),
-    ('mq', 1, 3),
-    ('eq', 1, 3),
-    ('qk', 3, 2),
-    ('il', 2, 2),
-    ('qk', 3, 3),
-    ('il', 2, 3),
-    ('mz', 0, 1),
-    ('ez', 0, 1),
-    ('mz', 0, 2),
-    ('ez', 0, 2),
-    ('qk', 2, 2),
-    ('qk', 2, 3),
-    ('mz', 0, 3),
-    ('ez', 0, 3),
-    ('mq', 3, 0),
-    ('eq', 3, 0),
-    ('mq', 3, 1),
-    ('eq', 3, 1),
-    ('mq', 3, 2),
-    ('eq', 3, 2),
-    ('mq', 3, 3),
-    ('eq', 3, 3),
-    ('mz', 1, 0),
-    ('ez', 1, 0),
-    ('mz', 1, 1),
-    ('ez', 1, 1),
-    ('mz', 1, 2),
-    ('ez', 1, 2),
-    ('mz', 1, 3),
-    ('ez', 1, 3),
-]
+        by_letter = {"tensor": tensor, "empty": empty, "quantise": quantise}
+        by_indices = {"widen": widen, "sort": sort_x, "bias_gain": bias_gain, "interleave": interleave}
+        for kind, letter, idx in program_order():
+            if kind in by_letter:
+                by_letter[kind](letter, idx)
+            else:
+                by_indices[kind](*idx)

from contextlib import ExitStack

import concourse.mybir as mybir
from concourse.masks import make_identity

T, C, D, R = 2048, 1024, 512, 512
FLOPS = 2 * T * C * 3 * D + 2 * R * T * 2 * D

F32 = mybir.dt.float32
BF16 = mybir.dt.bfloat16
I32 = mybir.dt.int32
U32 = mybir.dt.uint32
U8 = mybir.dt.uint8
FP8 = mybir.dt.float8_e4m3fn
FP8X4 = mybir.dt.float8_e4m3fn_x4
FP4X4 = mybir.dt.float4_e2m1fn_x4
ADD = mybir.AluOpType.add
MULT = mybir.AluOpType.mult
COPY = mybir.ActivationFunctionType.Copy

P = 128
KP = 512
HALF = KP // 2
GROUPS = T // KP
PASSES = C // KP
BLOCKS = C // P
TILES = D // P
TURNED = 2

WIDEN_ON_VECTOR = (6, 7, 8)
SORTED_GROUPS = (0, 2, 3)
SHARED_BANKS = 5

LOADS = (
    ("w", 4, 2),
    ("x", 0, 0, 0, 2),
    ("w", 6, 2),
    ("x", 0, 0, 2, 2),
    ("x", 0, 1, 0, 2),
    ("x", 0, 1, 2, 2),
    ("x", 1, 0, 0, 4),
    ("x", 1, 1, 0, 4),
    ("w", 8, 4),
    ("x", 2, 0, 0, 4),
    ("w", 0, 4),
    ("x", 2, 1, 0, 4),
    ("x", 3, 0, 0, 4),
    ("x", 3, 1, 0, 4),
)

TENSOR_ORDER = """
U*3 G0 G1 W1*3 X0*4 X1*4 W1 B K00*3 W2*4 X2*4 T00 K00 W0*4 K11*4 K10*4 K20*3 T11*2 T10*2 X3*4 T00
K01*4 K20 K30*4 Q2*2 Q3*4 K21*4 T01*2 Q1*4 K31*4 Q2*2 Z0*4 Q0*4 Z1*4
"""

WIDEN_LEAD = 10
SORT_LEAD = 12
BIAS_GAIN_LEAD = 8
QUANTISE_LAG = 3
INTERLEAVE_LAG = 5
INTERLEAVE_STEP = 5
INTERLEAVED_QUANTISE_LAG = 6


def tensor_items():
    seen = {}
    items = []
    for word in TENSOR_ORDER.split():
        name, count = (word + "*1").split("*")[:2]
        letter, digits = name[0], [int(d) for d in name[1:]]
        for n in range(seen.get(name, 0), seen.get(name, 0) + int(count)):
            if letter == "W":
                items.append((letter, (TILES * digits[0] + n,)))
            elif letter == "X":
                items.append((letter, (digits[0],) + divmod(n, 2)))
            elif letter in "KTQZ":
                items.append((letter, tuple(digits) + (n,)))
            else:
                items.append((letter, tuple(digits)))
        seen[name] = seen.get(name, 0) + int(count)
    return items


def program_order():
    timed = []
    clock = 0
    for n, (letter, idx) in enumerate(tensor_items()):
        if letter == "W":
            timed.append((clock - WIDEN_LEAD, n, 0, ("widen", letter, idx)))
        if letter == "X" and idx[0] in SORTED_GROUPS:
            timed.append((clock - SORT_LEAD, n, 0, ("sort", letter, idx)))
        if letter == "K" and idx[0] >= TURNED:
            timed.append((clock - BIAS_GAIN_LEAD, n, 0, ("bias_gain", letter, idx)))
        timed.append((clock, n, 1, ("tensor", letter, idx)))
        if letter != "U":
            timed.append((clock, n, 2, ("empty", letter, idx)))
        clock += {"K": PASSES, "Q": PASSES, "Z": GROUPS}.get(letter, 1)
        if letter in "WXT":
            timed.append((clock + QUANTISE_LAG, n, 3, ("quantise", letter, idx)))
        if letter == "K" and idx[0] >= TURNED and idx[2] == TILES - 1:
            for lo in range(2):
                at = clock + INTERLEAVE_LAG + INTERLEAVE_STEP * lo
                timed.append((at, n, 3, ("interleave", "T", idx[:2] + (lo,))))
                timed.append((at + INTERLEAVED_QUANTISE_LAG, n, 4, ("quantise", "T", idx[:2] + (lo,))))
    return [entry[3] for entry in sorted(timed, key=lambda entry: entry[:3])]


def tile_qkv_token_compression_d4_kernel(
    tc, x, w_bytes, w_scale, bias, gain, e_words, e_scales, out_q, out_k, out_v
):
    nc = tc.nc
    turned_tokens = TURNED * KP
    with ExitStack() as ctx:
        keep = ctx.enter_context(tc.tile_pool(name="keep", bufs=1))
        stage = ctx.enter_context(tc.tile_pool(name="stage", bufs=3))
        psum = ctx.enter_context(tc.psum_pool(name="psum", bufs=8))
        ctx.enter_context(tc.manual_schedule())

        ident = keep.tile([P, P], F32, name="ident")
        pick = keep.tile([P, 2 * TILES], BF16, name="pick")
        ones = keep.tile([P, KP], BF16, name="ones")
        rows = keep.tile([P, turned_tokens + P], BF16, name="rows")
        gain_rows = keep.tile([P, TURNED, KP], BF16, name="gain_rows")
        gain_raw = keep.tile([P, GROUPS - TURNED, 4], BF16, name="gain_raw")
        gain_cols = keep.tile([P, GROUPS - TURNED, 4], F32, name="gain_cols")
        bias_rows = keep.tile([P, 3, D], BF16, name="bias_rows")
        bias_cols = keep.tile([P, 2, TILES], F32, name="bias_cols")
        scale_all = keep.tile([P, 3 * TILES * BLOCKS], F32, name="scale_all")
        e_codes = keep.tile([P, GROUPS, 2 * R], U8, name="e_codes", align_bytes=256)
        e_plane = keep.tile([P, GROUPS, R], U8, name="e_plane", align_bytes=256)
        x_codes = keep.tile([P, GROUPS, PASSES, KP], U32, name="x_codes", align_bytes=256)
        x_plane = keep.tile([P, GROUPS, PASSES, KP], U8, name="x_plane", align_bytes=256)
        w_codes = keep.tile([P, 3, PASSES, D], U32, name="w_codes", align_bytes=256)
        w_plane = keep.tile([P, 3, PASSES, D], U8, name="w_plane", align_bytes=256)
        kv_codes = keep.tile([P, GROUPS, 2, D], U32, name="kv_codes", align_bytes=256)
        kv_plane = keep.tile([P, GROUPS, 2, D], U8, name="kv_plane", align_bytes=256)

        x_raw, w_raw, x_sorted, w_wide, banks, grouped = {}, {}, {}, {}, {}, {}
        kv_rows, kv_planes, bias_gains, q_out = {}, {}, {}, {}
        shared = [item for item in tensor_items() if item[0] in "WXT"][0:SHARED_BANKS:2]

        def load_x(g, k, first, count):
            if (g, k) not in x_raw:
                x_raw[g, k] = keep.tile([P, 4, KP], BF16, name="x_raw_%d_%d" % (g, k))
            src = x[g * KP : (g + 1) * KP, k * KP : (k + 1) * KP].rearrange("(p t) c -> p t c", t=4)
            nc.sync.dma_start(out=x_raw[g, k][:, first : first + count], in_=src[:, first : first + count])

        def load_w(first, count):
            tile = keep.tile([P, count, C], U8, name="w_raw_%d" % first)
            src = w_bytes[first * P : (first + count) * P, :].rearrange("(i p) c -> p i c", p=P)
            nc.sync.dma_start(out=tile[:], in_=src)
            for i in range(count):
                w_raw[first + i] = tile[:, i, :]

        def widen(i):
            wide = stage.tile([P, C], BF16, name="w_wide", bufs=6)
            w_wide[i] = wide
            for j in range(BLOCKS):
                cols = slice(j * P, (j + 1) * P)
                scale = scale_all[:, i * BLOCKS + j : i * BLOCKS + j + 1]
                src = w_raw[i][:, cols].bitcast(FP8)
                if j < WIDEN_ON_VECTOR[i // TILES]:
                    nc.vector.tensor_scalar(out=wide[:, cols], in0=src, scalar1=scale, scalar2=None, op0=MULT)
                else:
                    nc.scalar.activation(out=wide[:, cols], in_=src, func=COPY, scale=scale)

        def sort_x(g, k, h):
            tile = stage.tile([P, 2, 2, P], F32, name="x_sorted", bufs=6)
            x_sorted[g, k, h] = tile
            pairs = x_raw[g, k][:, 2 * h : 2 * h + 2, :].rearrange("p e c -> p (e c)").bitcast(F32)
            nc.scalar.copy(out=tile[:], in_=pairs.rearrange("p (e q u) -> p e u q", e=2, u=2))

        def bias_gain(g, h, t):
            tile = stage.tile([P, D], F32, name="bias_gain", bufs=6)
            bias_gains[g, h, t] = tile
            scale = gain_cols[:, g - TURNED, t : t + 1]
            nc.scalar.activation(out=tile[:], in_=bias_rows[:, 1 + h, :], func=COPY, scale=scale)

        def turn(letter, idx):
            bank = psum.tile([P, 2, 2, P], F32, name="bank")
            for a in range(2):
                for u in range(2):
                    if letter == "W":
                        src = w_wide[idx[0]][:].bitcast(F32)[:, HALF * a + u : HALF * (a + 1) : 2]
                    elif letter == "X" and idx in x_sorted:
                        src = x_sorted[idx][:, a, u, :]
                    elif letter == "X":
                        g, k, h = idx
                        src = x_raw[g, k][:, 2 * h + a, :].bitcast(F32)[:, u:HALF:2]
                    else:
                        g, h, lo = idx
                        src = kv_rows[g, h, 2 * lo + a][:].bitcast(F32)[:, u * P : (u + 1) * P]
                    nc.tensor.transpose(bank[:, a, u, :], src, ident[:])
            return bank

        def product(stationary, moving):
            bank = psum.tile([P, KP], F32, name="bank")
            for k, ((a, a_plane), (b, b_plane)) in enumerate(zip(stationary, moving)):
                nc.tensor.matmul_mx(
                    out=bank[:],
                    lhsT=a,
                    lhsT_scale=a_plane,
                    rhs=b,
                    rhs_scale=b_plane,
                    start=(k == 0),
                    stop=(k == len(moving) - 1),
                )
            return bank

        def x_operand(g, cols):
            return [(x_codes[:, g, k, cols].bitcast(FP8X4), x_plane[:, g, k, cols]) for k in range(PASSES)]

        def w_operand(part, cols):
            return [(w_codes[:, part, k, cols].bitcast(FP8X4), w_plane[:, part, k, cols]) for k in range(PASSES)]

        def tensor(letter, idx):
            everything = slice(0, KP)
            tile_cols = slice(idx[-1] * P, (idx[-1] + 1) * P) if letter in "KQZ" else None
            if letter in "WXT":
                bank = turn(letter, idx)
            elif letter == "Q":
                bank = product(x_operand(idx[0], tile_cols), w_operand(0, everything))
            elif letter == "K" and idx[0] >= TURNED:
                bank = product(x_operand(idx[0], tile_cols), w_operand(1 + idx[1], everything))
            elif letter == "K":
                bank = product(w_operand(1 + idx[1], tile_cols), x_operand(idx[0], everything))
            elif letter == "Z":
                h, r = idx
                words = slice(2 * r * P, 2 * (r + 1) * P)
                e_operand = [(e_codes[:, g, words].bitcast(FP4X4), e_plane[:, g, tile_cols]) for g in range(GROUPS)]
                kv_operand = [(kv_codes[:, g, h, :].bitcast(FP8X4), kv_plane[:, g, h, :]) for g in range(GROUPS)]
                bank = product(e_operand, kv_operand)
            elif letter == "G":
                bank = psum.tile([P, KP], BF16, name="bank")
                src = rows[:, idx[0] * KP : (idx[0] + 1) * KP].rearrange("r (p u e) -> r u p e", u=2, e=2)
                nc.tensor.matmul(bank[:], lhsT=ones[:, :P], rhs=src, start=True, stop=True)
            elif letter == "B":
                bank = psum.tile([P, 2 * TILES], F32, name="bank")
                nc.tensor.matmul(bank[:], lhsT=rows[:, turned_tokens:], rhs=pick[:], start=True, stop=True)
            else:
                bank = psum.tile([P, KP], F32, name="bank")
                nc.tensor.matmul(bank[:], lhsT=ones[:, :P], rhs=ones[:], start=True, stop=True)
            banks[letter, idx] = bank

        def empty_turned(letter, idx):
            tile = stage.tile([P, KP], F32, name="grouped", bufs=8, align_bytes=64)
            grouped[letter, idx] = tile
            if letter == "X" and idx[0] < TURNED:
                src = banks[letter, idx][:].rearrange("p a u n -> p n a u")
            else:
                src = banks[letter, idx][:].rearrange("p a u n -> p a n u")
            dst = tile[:].rearrange("p (a b c) -> p a b c", a=src.shape[1], b=src.shape[2])
            if (letter, idx) in shared:
                nc.vector.tensor_copy(out=dst, in_=src)
            else:
                nc.scalar.copy(out=dst, in_=src)

        def empty_kv(g, h, i):
            bank = banks["K", (g, h, i)]
            if g < TURNED:
                tile = stage.tile([P, KP], BF16, name="kv_rows", bufs=TURNED * 2 * TILES)
                kv_rows[g, h, i] = tile
                nc.vector.scalar_tensor_tensor(
                    out=tile[:], in0=bank[:], scalar=bias_cols[:, h, i : i + 1], in1=gain_rows[:, g, :], op0=ADD, op1=MULT
                )
            else:
                if i == 0:
                    kv_planes[g, h] = stage.tile([P, 4, D], BF16, name="kv_planes")
                nc.vector.scalar_tensor_tensor(
                    out=kv_planes[g, h][:, i, :],
                    in0=bank[:],
                    scalar=gain_cols[:, g - TURNED, i : i + 1],
                    in1=bias_gains[g, h, i][:],
                    op0=MULT,
                    op1=ADD,
                )

        def empty_q(g, j):
            u, a = divmod(j, 2)
            if a == 0:
                q_out[g, u] = stage.tile([P, 2, D], F32, name="q_out")
            nc.vector.tensor_tensor(out=q_out[g, u][:, a, :], in0=banks["Q", (g, j)][:], in1=bias_rows[:, 0, :], op=ADD)
            if a == 0:
                return
            group_rows = out_q[g * KP : (g + 1) * KP, :]
            if g < TURNED:
                dst = group_rows.rearrange("(a p u e) n -> u e p a n", a=2, u=2, e=2)
                for e in range(2):
                    nc.sync.dma_start(out=dst[u, e], in_=q_out[g, u][e:P:2])
            else:
                dst = group_rows.rearrange("(p u a) n -> u p a n", u=2, a=2)
                nc.sync.dma_start(out=dst[u], in_=q_out[g, u][:])

        def empty(letter, idx):
            bank = banks[letter, idx]
            if letter in "WXT":
                empty_turned(letter, idx)
            elif letter == "K":
                empty_kv(*idx)
            elif letter == "Q":
                empty_q(*idx)
            elif letter == "Z":
                h, r = idx
                tile = stage.tile([P, D], F32, name="z_out", bufs=4)
                nc.scalar.copy(out=tile[:], in_=bank[:])
                nc.sync.dma_start(out=(out_k, out_v)[h][r * P : (r + 1) * P, :], in_=tile[:])
            elif letter == "G":
                nc.scalar.copy(out=gain_rows[:, idx[0], :], in_=bank[:])
            else:
                nc.vector.tensor_copy(out=bias_cols[:].rearrange("p h i -> p (h i)"), in_=bank[:])
                nc.vector.tensor_copy(out=gain_cols[:], in_=gain_raw[:])

        def interleave(g, h, lo):
            tile = stage.tile([P, KP], F32, name="grouped", bufs=8, align_bytes=64)
            grouped["T", (g, h, lo)] = tile
            dst = tile[:].bitcast(BF16).rearrange("p (n t) -> p n t", t=4)
            src = kv_planes[g, h][:, :, HALF * lo : HALF * (lo + 1)].rearrange("p t n -> p n t")
            if (g, h) == (GROUPS - 1, 1):
                nc.vector.tensor_copy(out=dst, in_=src)
            else:
                nc.scalar.copy(out=dst, in_=src)

        def quantise(letter, idx):
            pairs = grouped[letter, idx]
            if letter == "W":
                part, i = divmod(idx[0], TILES)
                cols = slice(i * P, (i + 1) * P)
                jobs = [
                    (w_codes[:, part, k, cols], w_plane[:, part, k, cols], pairs[:, HALF * k : HALF * (k + 1)])
                    for k in range(PASSES)
                ]
            else:
                codes, plane = (x_codes, x_plane) if letter == "X" else (kv_codes, kv_plane)
                cols = slice(HALF * idx[2], HALF * (idx[2] + 1))
                jobs = [(codes[:, idx[0], idx[1], cols], plane[:, idx[0], idx[1], cols], pairs[:])]
            for codes_out, plane_out, src in jobs:
                nc.vector.quantize_mx(out=codes_out.bitcast(FP8X4), scales=plane_out, in_=src.bitcast(BF16))

        nc.sync.dma_start(out=scale_all[:], in_=w_scale.rearrange("i j -> (i j)").partition_broadcast(P))
        nc.vector.memset(ones[:], 1.0)
        nc.vector.memset(rows[:].bitcast(I32), 0)
        make_identity(nc, ident[:])
        nc.gpsimd.memset(e_plane[:].rearrange("p g n -> p (g n)").bitcast(U32), 0)
        nc.scalar.dma_start(out=rows[0:1, 0:turned_tokens], in_=gain[0:turned_tokens].rearrange("(o t) -> o t", o=1))
        nc.scalar.dma_start(out=rows[0 : 2 * TILES, turned_tokens:], in_=bias[D:].rearrange("(i p) -> i p", p=P))
        nc.scalar.dma_start(out=gain_raw[:], in_=gain[turned_tokens:].rearrange("(g p t) -> p g t", p=P, t=4))
        nc.scalar.copy(out=pick[:], in_=ident[:, 0 : 2 * TILES])
        for load in LOADS:
            if load[0] == "w":
                load_w(*load[1:])
            else:
                load_x(*load[1:])
        nc.sync.dma_start(out=bias_rows[:].rearrange("p a n -> p (a n)"), in_=bias.partition_broadcast(P))
        nc.sync.dma_start(out=e_codes[:].bitcast(I32), in_=e_words.rearrange("g p n -> p g n").bitcast(I32))
        for q in range(4):
            nc.sync.dma_start(
                out=e_plane[32 * q : 32 * q + 4].bitcast(I32),
                in_=e_scales[:, 4 * q : 4 * q + 4, :].rearrange("g r n -> r g n").bitcast(I32),
            )

        by_letter = {"tensor": tensor, "empty": empty, "quantise": quantise}
        by_indices = {"widen": widen, "sort": sort_x, "bias_gain": bias_gain, "interleave": interleave}
        for kind, letter, idx in program_order():
            if kind in by_letter:
                by_letter[kind](letter, idx)
            else:
                by_indices[kind](*idx)
